import numpy as np
import ml_dtypes


def mxq(x, axis, fmt="e4m3"):
    dtype, down = {"e4m3": (ml_dtypes.float8_e4m3fn, 7), "e5m2": (ml_dtypes.float8_e5m2, 14)}[fmt]
    v = np.moveaxis(np.asarray(x, np.float32).astype(ml_dtypes.bfloat16).astype(np.float64), axis, -1)
    blocks = v.reshape(v.shape[:-1] + (-1, 32))
    amax = np.abs(blocks).max(-1, keepdims=True)
    byte = np.maximum(np.where(amax > 0, np.frexp(amax)[1] - 1 + 127, 0) - down, 1)
    scale = np.exp2(byte - 127.0)
    codes = (blocks / scale).astype(np.float32).astype(dtype).astype(np.float64)
    return np.moveaxis((codes * scale).reshape(v.shape), -1, axis)


WIDE = False


def mx_kscale(k):
    if not WIDE:
        return np.ones(k)
    levels = np.array([10, -10, 5, -5, 0])
    if k % 512:
        return np.exp2(np.random.permutation(np.resize(levels, k // 32))).repeat(32)
    a = np.empty((k // 512, 16))
    for p in range(k // 512):
        a[p, :8] = np.random.permutation(np.resize(levels, 8))
        for g in range(8):
            far = levels[np.abs(levels - a[p, g]) >= 10]
            a[p, g + 8] = far[np.random.randint(len(far))]
    return np.exp2(a.ravel()).repeat(32)


BF16 = ml_dtypes.bfloat16


def bf(x):
    return np.asarray(x, np.float32).astype(BF16)


def f64(x):
    return np.asarray(x).astype(np.float64)


E2M1 = np.array([0.0, 0.5, 1.0, 1.5, 2.0, 3.0, 4.0, 6.0, -0.0, -0.5, -1.0, -1.5, -2.0, -3.0, -4.0, -6.0])


def pack_weight(w, fmt):
    k, n = w.shape
    w = f64(bf(w)).reshape(k // 32, 32, n)
    amax = np.abs(w).max(1)
    if fmt == "e4m3":
        byte = np.frexp(amax)[1] - 1 + 127 - 7
    else:
        mant, ex = np.frexp(amax / 6.0)
        byte = np.where(mant > 0.5, ex, ex - 1) + 127
    byte = np.clip(np.where(amax > 0, byte, 1), 1, 254)
    scaled = (w * np.exp2(127.0 - byte)[:, None, :]).reshape(k, n).astype(np.float32)
    by_word = np.ascontiguousarray(scaled.reshape(k // 512, 128, 4, n).transpose(0, 1, 3, 2))
    if fmt == "e4m3":
        words = by_word.astype(ml_dtypes.float8_e4m3fn).view(np.uint8)
    else:
        c = by_word.astype(ml_dtypes.float4_e2m1fn).view(np.uint8) & 0xF
        words = c[..., 0::2] | (c[..., 1::2] << 4)
    return np.ascontiguousarray(words), np.ascontiguousarray(byte.astype(np.uint8).reshape(k // 512, 16, n))


def unpack_weight(words, scales, fmt):
    g, p, n, _ = words.shape
    if fmt == "e4m3":
        vals = np.ascontiguousarray(words).view(ml_dtypes.float8_e4m3fn).astype(np.float64)
    else:
        nib = np.empty((g, p, n, 4), np.uint8)
        nib[..., 0::2] = words & 0xF
        nib[..., 1::2] = words >> 4
        vals = E2M1[nib]
    vals = vals * np.repeat(np.exp2(scales.astype(np.float64) - 127.0), 8, axis=1)[..., None]
    return vals.transpose(0, 1, 3, 2).reshape(g * 512, n)
def pack4(w):
    words, scales = pack_weight(w, "e2m1")
    return words.reshape(words.shape[0], 128, -1), scales


def unpack4(words, scales):
    return unpack_weight(words.reshape(words.shape[0], 128, -1, 2), scales, "e2m1")


def planes(Y):
    n, m = Y.shape
    b = f64(bf(Y)).reshape(n // 32, 32, m)
    amax = np.abs(b).max(1)
    byte = np.clip(np.where(amax > 0, np.frexp(amax)[1] - 1 + 127 - 7, 1), 1, 254)
    codes = (b * np.exp2(127.0 - byte)[:, None, :]).reshape(n, m).astype(np.float32).astype(ml_dtypes.float8_e4m3fn).view(np.uint8)
    words = codes.reshape(n // 512, 128, 4, m).transpose(0, 1, 3, 2)
    return np.ascontiguousarray(words), np.ascontiguousarray(byte.astype(np.uint8).reshape(n // 512, 16, m))


N = 1024

SPREAD = 0.8
REST = 0.35

def symmetric_noise():
    a = np.random.randn(N, N)
    return (a + a.T) / np.sqrt(2.0)

def setup_inputs():
    s, t, u = mx_kscale(N), mx_kscale(N), mx_kscale(N)
    P = symmetric_noise()
    F0 = REST * symmetric_noise() / np.sqrt(N)
    e = np.sign(np.random.randn(N)) * np.exp(0.4 * np.random.randn(N))
    d = f64(bf(1.0 + 0.1 * np.random.randn(N)))
    W = REST * np.random.randn(N, N) / np.sqrt(N)
    w_words, w_scales = pack4(W / s[:, None])
    L = np.linalg.inv(np.diag(d) + unpack4(w_words, w_scales) * s[:, None])
    omega = 0.5 * np.exp(SPREAD * np.random.randn(N))
    return {"p_mat": bf(P * t[:, None] * s[None, :]),
            "w_words": w_words, "w_scales": w_scales, "d": bf(d / s),
            "f_mat": bf(F0 * u[:, None] / t[None, :]), "e": bf(e * u / t),
            "l_mat": bf(L / u[None, :]), "omega": bf(omega)}

def reference(p_mat, w_words, w_scales, d, f_mat, e, l_mat, omega):
    P, F0, L = f64(p_mat), f64(f_mat), f64(l_mat)
    W = unpack4(w_words, w_scales)
    A = P * f64(d)[None, :] + (mxq(P, 1, "e4m3") @ W)
    B = f64(e)[:, None] * A + (mxq(F0, 1, "e4m3") @ mxq(A, 0, "e4m3"))
    C = mxq(L, 1, "e4m3") @ mxq(B, 0, "e4m3")
    y = f64(omega)[:, None] * (C - C.T)
    Y = y.reshape(N, N)
    words, scales = planes(Y)
    return y, words, scales

@@ -1,0 +1,425 @@
+from contextlib import ExitStack
+
+import concourse.mybir as mybir
+from concourse.masks import make_identity
+
+N = 1024
+FLOPS = 3 * 2 * N * N * N
+
+F32 = mybir.dt.float32
+BF16 = mybir.dt.bfloat16
+I32 = mybir.dt.int32
+U32 = mybir.dt.uint32
+U8 = mybir.dt.uint8
+FP8X4 = mybir.dt.float8_e4m3fn_x4
+FP4X4 = mybir.dt.float4_e2m1fn_x4
+ALU = mybir.AluOpType
+ACT = mybir.ActivationFunctionType
+
+PART = 128
+PACK = 4
+HALF = 512
+TILES = 8
+
+
+def tile_weighted_diis_error_k1_kernel(
+    tc, p_mat, w_words, w_scales, d, f_mat, e, l_mat, omega, out_0, out_1, out_2
+):
+    nc = tc.nc
+    with ExitStack() as ctx:
+        keep = ctx.enter_context(tc.tile_pool(name="keep", bufs=1))
+        work = ctx.enter_context(tc.tile_pool(name="work", bufs=2))
+        psum = ctx.enter_context(tc.psum_pool(name="psum", bufs=1))
+        ctx.enter_context(tc.manual_schedule())
+
+        def kept(name, shape, dtype):
+            return keep.tile(shape, dtype, name=name, align_bytes=64)
+
+        def staged(tag, shape, dtype, bufs):
+            return work.tile(shape, dtype, name=tag, tag=tag, bufs=bufs, align_bytes=64)
+
+        def bank(index):
+            return psum.tile([PART, HALF], F32, name="bank%d" % index, tag="bank%d" % index)
+
+        def by_slot(mat, g):
+            return mat[HALF * g : HALF * (g + 1), :].rearrange("(p t) k -> p t k", t=PACK)
+
+        def quantize(name, src):
+            width = src.shape[1] // PACK
+            codes = kept(name + "_codes", [PART, width], U32)
+            scales = kept(name + "_scales", [PART, width], U8)
+            nc.vector.quantize_mx(out=codes[:].bitcast(FP8X4), scales=scales[:], in_=src)
+            return codes, scales
+
+        w_plane = kept("w_plane", [PART, 2, N], U8)
+        nc.vector.memset(w_plane[:].rearrange("p g n -> p (g n)").bitcast(I32), 0)
+        d_rows = kept("d_rows", [PART, 8], BF16)
+        nc.scalar.dma_start(out=d_rows[:], in_=d.rearrange("(p c) -> p c", c=8))
+        p_raw = [kept("p_raw%d" % r, [PART, N], BF16) for r in range(TILES)]
+        w_codes = [kept("w_codes%d" % h, [PART, 2, N], U8) for h in range(2)]
+
+        def load_p(r):
+            nc.sync.dma_start(out=p_raw[r][:], in_=by_slot(p_mat, r // PACK)[:, r % PACK, :])
+
+        def load_w(h):
+            nc.sync.dma_start(
+                out=w_codes[h][:].bitcast(I32),
+                in_=w_words.rearrange("g p n -> p g n")[:, :, N * h : N * (h + 1)].bitcast(I32),
+            )
+
+        load_p(0)
+        load_p(1)
+        load_w(0)
+        for q in range(4):
+            nc.scalar.dma_start(
+                out=w_plane[32 * q : 32 * q + 4, :, :].bitcast(I32),
+                in_=w_scales.rearrange("g r n -> r g n")[4 * q : 4 * q + 4, :, :].bitcast(I32),
+            )
+        ident = kept("ident", [PART, PART], F32)
+        make_identity(nc, ident[:])
+        e_cols = kept("e_cols", [PART, 2, PACK], BF16)
+        nc.gpsimd.dma_start(out=e_cols[:], in_=e.rearrange("(g p t) -> p g t", g=2, t=PACK))
+        omega_bf = kept("omega_bf", [PART, 2, PACK], BF16)
+        nc.gpsimd.dma_start(out=omega_bf[:], in_=omega.rearrange("(g p t) -> p g t", g=2, t=PACK))
+        for r in range(2, TILES):
+            load_p(r)
+        load_w(1)
+        raw = {}
+        for name, mat in (("f", f_mat), ("l", l_mat)):
+            for g in range(2):
+                slab = staged("slab", [PART, PACK, N], BF16, 4)
+                nc.sync.dma_start(out=slab[:], in_=by_slot(mat, g))
+                raw[name, g] = slab
+
+        d_bank = bank(7)
+        d_words = d_rows[:].bitcast(F32)
+        for c in range(4):
+            nc.tensor.transpose(
+                d_bank[:, PART * c : PART * (c + 1)], d_words[:, c : c + 1].to_broadcast([PART, PART]), ident[:]
+            )
+        d_all = kept("d_all", [PART, N], BF16)
+        nc.vector.tensor_copy(
+            out=d_all[:].bitcast(F32).rearrange("p (n c) -> p n c", c=4),
+            in_=d_bank[:].rearrange("p (c n) -> p n c", c=4),
+        )
+        omega_cols = kept("omega_cols", [PART, 2, PACK], F32)
+        omega_neg = kept("omega_neg", [PART, 2, PACK], F32)
+
+        turned, pq, fq, lq, nlq, aq, bq = {}, {}, {}, {}, {}, {}, {}
+        pd, acc, a_full, b_rows, inter, l_turned, y_full = {}, {}, {}, {}, {}, {}, {}
+
+        def raw_rows(name, r):
+            return p_raw[r][:] if name == "p" else raw[name, r // PACK][:, r % PACK, :]
+
+        def turn(name, r, index):
+            words = raw_rows(name, r).bitcast(F32)
+            dst = bank(index)
+            for c in range(2):
+                for u in range(2):
+                    j = 2 * c + u
+                    nc.tensor.transpose(
+                        dst[:, PART * j : PART * (j + 1)], words[:, 256 * c + u : 256 * (c + 1) : 2], ident[:]
+                    )
+            acc["t", name, r] = dst
+
+        def empty_turned(name, r):
+            src = acc["t", name, r][:].rearrange("p (c u m) -> p c m u", c=2, u=2)
+            if name == "l":
+                h, t = divmod(r, PACK)
+                if t == 0:
+                    l_turned[h] = staged("l_turned", [PART, 2 * HALF * PACK], BF16, 2)
+                dst = l_turned[h][:].bitcast(F32).rearrange("p (c t m u) -> p t c m u", c=2, t=PACK, u=2)[:, t]
+            else:
+                xt = staged("turned", [PART, 2 * PART * PACK], BF16, 4)
+                turned[name, r] = xt
+                dst = xt[:].bitcast(F32).rearrange("p (c m u) -> p c m u", c=2, u=2)
+            nc.scalar.copy(out=dst, in_=src)
+
+        def quantize_turned(name, r):
+            (pq if name == "p" else fq)[r] = quantize("%sq%d" % (name, r), turned[name, r][:])
+
+        def quantize_l(h):
+            lq[h] = quantize("lq%d" % h, l_turned[h][:])
+
+        def negate_l(h):
+            neg = staged("l_neg", [PART, 2 * HALF * PACK], BF16, 1)
+            nc.vector.tensor_scalar(out=neg[:], in0=l_turned[h][:], scalar1=-1.0, scalar2=None, op0=ALU.mult)
+            turned["n", h] = neg
+
+        def quantize_negated(h):
+            nlq[h] = quantize("nlq%d" % h, turned["n", h][:])
+
+        def scale_p(r, h):
+            cols = slice(HALF * h, HALF * (h + 1))
+            prod = staged("pd", [PART, HALF], F32, 4)
+            nc.vector.tensor_tensor(out=prod[:], in0=p_raw[r][:, cols], in1=d_all[:, cols], op=ALU.mult)
+            pd[r, h] = prod
+
+        def mx(dst, lhs, lhs_col, rhs, rhs_col, start, stop):
+            lcols = slice(lhs_col, lhs_col + PART)
+            rcols = slice(rhs_col, rhs_col + HALF)
+            nc.tensor.matmul_mx(
+                out=dst[:],
+                lhsT=lhs[0][:, lcols].bitcast(FP8X4),
+                lhsT_scale=lhs[1][:, lcols],
+                rhs=rhs[0][:, rcols].bitcast(FP8X4),
+                rhs_scale=rhs[1][:, rcols],
+                start=start,
+                stop=stop,
+            )
+
+        def product_a(r, h, index):
+            dst = bank(index)
+            for c in range(2):
+                lcols = slice(PART * c, PART * (c + 1))
+                nc.tensor.matmul_mx(
+                    out=dst[:],
+                    lhsT=pq[r][0][:, lcols].bitcast(FP8X4),
+                    lhsT_scale=pq[r][1][:, lcols],
+                    rhs=w_codes[h][:, c, :].bitcast(FP4X4),
+                    rhs_scale=w_plane[:, c, HALF * h : HALF * (h + 1)],
+                    start=(c == 0),
+                    stop=(c == 1),
+                )
+            acc["a", r, h] = dst
+
+        def finish_a(r, h):
+            g, t = divmod(r, PACK)
+            if t == 0:
+                a_full[g, h] = kept("a_full%d%d" % (g, h), [PART, PACK, HALF], F32)
+            nc.vector.tensor_tensor(out=a_full[g, h][:, t, :], in0=acc["a", r, h][:], in1=pd[r, h][:], op=ALU.add)
+
+        def product_b(r, h, index):
+            dst = bank(index)
+            for c in range(2):
+                mx(dst, fq[r], PART * c, aq[c, h], 0, c == 0, c == 1)
+            acc["b", r, h] = dst
+
+        def finish_b(r, h):
+            g, t = divmod(r, PACK)
+            if t == 0:
+                b_rows[g, h] = staged("b_rows", [PART, PACK, HALF], BF16, 2)
+            nc.vector.scalar_tensor_tensor(
+                out=b_rows[g, h][:, t, :],
+                in0=a_full[g, h][:, t, :],
+                scalar=e_cols[:, g, t : t + 1],
+                in1=acc["b", r, h][:],
+                op0=ALU.mult,
+                op1=ALU.add,
+            )
+
+        def interleave(kind, g, h, part, copy):
+            if part == 0:
+                inter[kind, g, h] = staged("inter", [PART, HALF, PACK], BF16, 4)
+            src = {"a": a_full, "b": b_rows, "y": y_full}[kind][g, h][:].rearrange("p t (m s) -> p m t s", s=PACK)
+            pattern = "p (s m) t -> p m t s" if kind == "b" else "p (m s) t -> p m t s"
+            dst = inter[kind, g, h][:].rearrange(pattern, s=PACK)
+            ms = slice(64 * part, 64 * (part + 1))
+            copy(out=dst[:, ms], in_=src[:, ms])
+
+        def quantize_inter(kind, g, h):
+            src = inter[kind, g, h][:].rearrange("p n t -> p (n t)")
+            (aq if kind == "a" else bq)[g, h] = quantize("%sq%d%d" % (kind, g, h), src)
+
+        y_scales = kept("y_scales", [PART, N], U8)
+        y_codes = {}
+
+        def open_y(g, h, first):
+            for t in range(PACK):
+                acc["y", g, h, t] = bank(first + t)
+
+        def pass_lb(g, h, t, c, start=False, stop=False):
+            mx(acc["y", g, h, t], lq[g], HALF * c + PART * t, bq[c, h], 0, start, stop)
+
+        def pass_bl(g, h, t, c, start=False, stop=False):
+            mx(acc["y", g, h, t], bq[c, g], PART * t, nlq[h], HALF * c, start, stop)
+
+        def weight_y(g, h, t, weights):
+            if t == 0:
+                y_full[g, h] = staged("slab", [PART, PACK, HALF], F32, 4)
+            nc.scalar.activation(
+                out=y_full[g, h][:, t, :].rearrange("p (m s) -> p m s", s=PACK),
+                in_=acc["y", g, h, t][:].rearrange("p (s m) -> p m s", s=PACK),
+                func=ACT.Copy,
+                scale=weights[:, g, t : t + 1],
+            )
+            store_y(g, h, t)
+
+        def weight_plain(plain, g, h, t):
+            if t == 0:
+                y_full[g, h] = staged("slab", [PART, PACK, HALF], F32, 4)
+            nc.vector.tensor_scalar(
+                out=y_full[g, h][:, t, :].rearrange("p (n i s) -> p n s i", i=2, s=PACK),
+                in0=plain[:, t, :].rearrange("p (s n i) -> p n s i", i=2, s=PACK),
+                scalar1=omega_cols[:, g, t : t + 1],
+                scalar2=None,
+                op0=ALU.mult,
+            )
+            store_y(g, h, t)
+
+        def store_y(g, h, t):
+            if t % 2 == 1:
+                pair = slice(t - 1, t + 1)
+                nc.sync.dma_start(
+                    out=by_slot(out_0, g)[:, pair, HALF * h : HALF * (h + 1)], in_=y_full[g, h][:, pair, :]
+                )
+
+        def quantize_y(g, h):
+            codes = kept("y_codes%d%d" % (g, h), [PART, HALF], U32)
+            nc.vector.quantize_mx(
+                out=codes[:].bitcast(FP8X4),
+                scales=y_scales[4 * g :, HALF * h : HALF * (h + 1)],
+                in_=inter["y", g, h][:].rearrange("p n t -> p (n t)"),
+            )
+            y_codes[g, h] = codes
+
+        def store_words(g, h):
+            words = out_1[g].rearrange("p m t -> p (m t)")
+            nc.sync.dma_start(
+                out=words[:, PACK * HALF * h : PACK * HALF * (h + 1)].bitcast(I32), in_=y_codes[g, h][:].bitcast(I32)
+            )
+
+        def store_scales():
+            for q in range(4):
+                (nc.sync if q % 2 == 0 else nc.scalar).dma_start(
+                    out=out_2[:, 4 * q : 4 * q + 4, :].bitcast(I32),
+                    in_=y_scales[32 * q : 32 * q + 8, :].bitcast(I32),
+                )
+
+        runs = [(name, 2 * j) for name in "pfl" for j in range(4)]
+        jobs = [("a", 2 * j, 0) for j in range(4)] + [("a", 2 * j, 1) for j in range(4)] + [("b", 0, 0)]
+        act_extra = {
+            3: ("a", 0, 0, 0), 4: ("a", 0, 0, 1), 5: ("a", 1, 0, 0), 6: ("a", 1, 0, 1),
+            7: ("a", 0, 1, 0), 8: ("a", 0, 1, 1), 9: ("a", 1, 1, 0),
+        }
+
+        def turn_pair(name, r0, first):
+            for k in range(2):
+                turn(name, r0 + k, first + k)
+            for k in range(2):
+                empty_turned(name, r0 + k)
+
+        def b_pair(r0, h, first):
+            for k in range(2):
+                product_b(r0 + k, h, first + k)
+
+        def finish_b_pair(r0, h):
+            for k in range(2):
+                finish_b(r0 + k, h)
+
+        for s in range(10):
+            name, r0 = runs[s]
+            turn_pair(name, r0, 2 * (s % 2))
+            if s == 2:
+                nc.scalar.activation(out=omega_cols[:], in_=omega_bf[:], func=ACT.Copy)
+                nc.scalar.activation(out=omega_neg[:], in_=omega_bf[:], func=ACT.Copy, scale=-1.0)
+            if s in act_extra:
+                interleave(*act_extra[s], nc.scalar.copy)
+            if s < 8:
+                for k in range(2):
+                    scale_p(jobs[s][1] + k, jobs[s][2])
+                for k in range(2):
+                    quantize_turned(name, r0 + k)
+            if s >= 1:
+                kind, j0, h = jobs[s - 1]
+                for k in range(2):
+                    (product_a if kind == "a" else product_b)(j0 + k, h, 4 + 2 * (s % 2) + k)
+                for k in range(2):
+                    (finish_a if kind == "a" else finish_b)(j0 + k, h)
+            if s in act_extra and act_extra[s][3] == 1:
+                quantize_inter(*act_extra[s][:3])
+
+        act, vec = nc.scalar.copy, nc.vector.tensor_copy
+        interleave("a", 1, 1, 1, act)
+        b_pair(2, 0, 4)
+        finish_b_pair(2, 0)
+        b_pair(4, 0, 6)
+        interleave("b", 0, 0, 0, act)
+        interleave("b", 0, 0, 1, act)
+        finish_b_pair(4, 0)
+        quantize_inter("a", 1, 1)
+        b_pair(6, 0, 0)
+        finish_b_pair(6, 0)
+        interleave("b", 1, 0, 0, act)
+        interleave("b", 1, 0, 1, act)
+        turn_pair("l", 4, 2)
+        b_pair(0, 1, 4)
+        b_pair(2, 1, 6)
+        turn_pair("l", 6, 0)
+        negate_l(0)
+        quantize_l(0)
+        quantize_inter("b", 0, 0)
+        quantize_negated(0)
+        quantize_inter("b", 1, 0)
+        finish_b_pair(0, 1)
+        finish_b_pair(2, 1)
+        b_pair(4, 1, 2)
+        b_pair(6, 1, 0)
+        interleave("b", 0, 1, 0, act)
+        interleave("b", 0, 1, 1, act)
+        open_y(0, 0, 4)
+        for t in range(PACK):
+            pass_lb(0, 0, t, 0, start=True)
+            pass_bl(0, 0, t, 0)
+            pass_lb(0, 0, t, 1)
+            pass_bl(0, 0, t, 1, stop=True)
+        quantize_l(1)
+        finish_b_pair(4, 1)
+        finish_b_pair(6, 1)
+        for t in range(2):
+            weight_y(0, 0, t, omega_cols)
+        quantize_inter("b", 0, 1)
+        interleave("b", 1, 1, 0, act)
+        interleave("b", 1, 1, 1, vec)
+        negate_l(1)
+        quantize_inter("b", 1, 1)
+        quantize_negated(1)
+        for t in range(2, PACK):
+            weight_y(0, 0, t, omega_cols)
+        open_y(1, 0, 0)
+        for t in range(PACK):
+            pass_lb(1, 0, t, 0, start=True)
+            pass_lb(1, 0, t, 1)
+        for t in range(PACK):
+            pass_bl(1, 0, t, 0)
+        for t in range(PACK):
+            pass_bl(1, 0, t, 1, stop=True)
+        interleave("y", 0, 0, 0, act)
+        plain = staged("l_turned", [PART, PACK, HALF], F32, 2)
+        for t in range(PACK):
+            nc.scalar.copy(out=plain[:, t, :], in_=acc["y", 1, 0, t][:])
+        interleave("y", 0, 0, 1, vec)
+        for t in range(PACK):
+            weight_plain(plain, 1, 0, t)
+        quantize_y(0, 0)
+        open_y(1, 1, 4)
+        for t in range(PACK):
+            pass_lb(1, 1, t, 0, start=True)
+            pass_lb(1, 1, t, 1)
+        for t in range(PACK):
+            pass_bl(1, 1, t, 0)
+            pass_bl(1, 1, t, 1, stop=True)
+        for part in range(2):
+            interleave("y", 1, 0, part, vec)
+        store_words(0, 0)
+        open_y(0, 1, 0)
+        for s in range(PACK):
+            for t in range(PACK):
+                nc.tensor.transpose(
+                    acc["y", 0, 1, s][:, PART * t : PART * (t + 1)], plain[:, t, PART * s : PART * (s + 1)], ident[:]
+                )
+        for t in range(PACK):
+            weight_y(1, 1, t, omega_cols)
+        for t in range(PACK):
+            weight_y(0, 1, t, omega_neg)
+        interleave("y", 1, 1, 0, vec)
+        quantize_y(1, 0)
+        interleave("y", 1, 1, 1, vec)
+        store_words(1, 0)
+        quantize_y(1, 1)
+        store_words(1, 1)
+        interleave("y", 0, 1, 0, vec)
+        interleave("y", 0, 1, 1, vec)
+        quantize_y(0, 1)
+        store_words(0, 1)
+        store_scales()

@@ -51,15 +51,19 @@ def tile_weighted_diis_error_k1_kernel(
             nc.vector.quantize_mx(out=codes[:].bitcast(FP8X4), scales=scales[:], in_=src)
             return codes, scales
 
-        w_plane = kept("w_plane", [PART, 2, N], U8)
-        nc.vector.memset(w_plane[:].rearrange("p g n -> p (g n)").bitcast(I32), 0)
         d_rows = kept("d_rows", [PART, 8], BF16)
         nc.scalar.dma_start(out=d_rows[:], in_=d.rearrange("(p c) -> p c", c=8))
-        p_raw = [kept("p_raw%d" % r, [PART, N], BF16) for r in range(TILES)]
+        w_plane = kept("w_plane", [PART, 2, N], U8)
+        nc.vector.memset(w_plane[:].rearrange("p g n -> p (g n)").bitcast(I32), 0)
         w_codes = [kept("w_codes%d" % h, [PART, 2, N], U8) for h in range(2)]
+        p_raw = {}
 
-        def load_p(r):
-            nc.sync.dma_start(out=p_raw[r][:], in_=by_slot(p_mat, r // PACK)[:, r % PACK, :])
+        def load_p(r0, count):
+            rows = kept("p_raw%d" % r0, [PART, count, N], BF16)
+            g, t = divmod(r0, PACK)
+            nc.sync.dma_start(out=rows[:], in_=by_slot(p_mat, g)[:, t : t + count, :])
+            for k in range(count):
+                p_raw[r0 + k] = rows[:, k, :]
 
         def load_w(h):
             nc.sync.dma_start(
@@ -67,8 +71,9 @@ def tile_weighted_diis_error_k1_kernel(
                 in_=w_words.rearrange("g p n -> p g n")[:, :, N * h : N * (h + 1)].bitcast(I32),
             )
 
-        load_p(0)
-        load_p(1)
+        load_p(0, 1)
+        load_p(1, 1)
+        load_p(2, 2)
         load_w(0)
         for q in range(4):
             nc.scalar.dma_start(
@@ -77,12 +82,12 @@ def tile_weighted_diis_error_k1_kernel(
             )
         ident = kept("ident", [PART, PART], F32)
         make_identity(nc, ident[:])
-        e_cols = kept("e_cols", [PART, 2, PACK], BF16)
-        nc.gpsimd.dma_start(out=e_cols[:], in_=e.rearrange("(g p t) -> p g t", g=2, t=PACK))
         omega_bf = kept("omega_bf", [PART, 2, PACK], BF16)
         nc.gpsimd.dma_start(out=omega_bf[:], in_=omega.rearrange("(g p t) -> p g t", g=2, t=PACK))
-        for r in range(2, TILES):
-            load_p(r)
+        e_cols = kept("e_cols", [PART, 2, PACK], BF16)
+        nc.gpsimd.dma_start(out=e_cols[:], in_=e.rearrange("(g p t) -> p g t", g=2, t=PACK))
+        load_p(4, 2)
+        load_p(6, 2)
         load_w(1)
         raw = {}
         for name, mat in (("f", f_mat), ("l", l_mat)):
@@ -91,17 +96,6 @@ def tile_weighted_diis_error_k1_kernel(
                 nc.sync.dma_start(out=slab[:], in_=by_slot(mat, g))
                 raw[name, g] = slab
 
-        d_bank = bank(7)
-        d_words = d_rows[:].bitcast(F32)
-        for c in range(4):
-            nc.tensor.transpose(
-                d_bank[:, PART * c : PART * (c + 1)], d_words[:, c : c + 1].to_broadcast([PART, PART]), ident[:]
-            )
-        d_all = kept("d_all", [PART, N], BF16)
-        nc.vector.tensor_copy(
-            out=d_all[:].bitcast(F32).rearrange("p (n c) -> p n c", c=4),
-            in_=d_bank[:].rearrange("p (c n) -> p n c", c=4),
-        )
         omega_cols = kept("omega_cols", [PART, 2, PACK], F32)
         omega_neg = kept("omega_neg", [PART, 2, PACK], F32)
 
@@ -109,7 +103,7 @@ def tile_weighted_diis_error_k1_kernel(
         pd, acc, a_full, b_rows, inter, l_turned, y_full = {}, {}, {}, {}, {}, {}, {}
 
         def raw_rows(name, r):
-            return p_raw[r][:] if name == "p" else raw[name, r // PACK][:, r % PACK, :]
+            return p_raw[r] if name == "p" else raw[name, r // PACK][:, r % PACK, :]
 
         def turn(name, r, index):
             words = raw_rows(name, r).bitcast(F32)
@@ -130,13 +124,18 @@ def tile_weighted_diis_error_k1_kernel(
                     l_turned[h] = staged("l_turned", [PART, 2 * HALF * PACK], BF16, 2)
                 dst = l_turned[h][:].bitcast(F32).rearrange("p (c t m u) -> p t c m u", c=2, t=PACK, u=2)[:, t]
             else:
-                xt = staged("turned", [PART, 2 * PART * PACK], BF16, 4)
-                turned[name, r] = xt
-                dst = xt[:].bitcast(F32).rearrange("p (c m u) -> p c m u", c=2, u=2)
+                if r % 2 == 0:
+                    turned[name, r // 2] = staged("turned%d" % ((r // 2 + (4 if name == "f" else 0)) % 3), [PART, 4 * PART * PACK], BF16, 1)
+                dst = turned[name, r // 2][:].bitcast(F32).rearrange("p (k c m u) -> p k c m u", k=2, c=2, u=2)[:, r % 2]
             nc.scalar.copy(out=dst, in_=src)
 
-        def quantize_turned(name, r):
-            (pq if name == "p" else fq)[r] = quantize("%sq%d" % (name, r), turned[name, r][:])
+        def quantize_turned(name, r0, count):
+            k0 = r0 % 2
+            src = turned[name, r0 // 2][:, 2 * PART * PACK * k0 : 2 * PART * PACK * (k0 + count)]
+            codes, scales = quantize("%sq%d" % (name, r0), src)
+            for k in range(count):
+                cols = slice(2 * PART * k, 2 * PART * (k + 1))
+                (pq if name == "p" else fq)[r0 + k] = (codes[:, cols], scales[:, cols])
 
         def quantize_l(h):
             lq[h] = quantize("lq%d" % h, l_turned[h][:])
@@ -149,10 +148,10 @@ def tile_weighted_diis_error_k1_kernel(
         def quantize_negated(h):
             nlq[h] = quantize("nlq%d" % h, turned["n", h][:])
 
-        def scale_p(r, h):
+        def scale_p(r, h, engine, tag, bufs):
             cols = slice(HALF * h, HALF * (h + 1))
-            prod = staged("pd", [PART, HALF], F32, 4)
-            nc.vector.tensor_tensor(out=prod[:], in0=p_raw[r][:, cols], in1=d_all[:, cols], op=ALU.mult)
+            prod = staged(tag, [PART, HALF], F32, bufs)
+            engine.tensor_tensor(out=prod[:], in0=p_raw[r][:, cols], in1=d_all[:, cols], op=ALU.mult)
             pd[r, h] = prod
 
         def mx(dst, lhs, lhs_col, rhs, rhs_col, start, stop):
@@ -208,19 +207,32 @@ def tile_weighted_diis_error_k1_kernel(
                 op1=ALU.add,
             )
 
-        def interleave(kind, g, h, part, copy):
+        def interleave(kind, g, h, part, copy, cut=64):
             if part == 0:
                 inter[kind, g, h] = staged("inter", [PART, HALF, PACK], BF16, 4)
             src = {"a": a_full, "b": b_rows, "y": y_full}[kind][g, h][:].rearrange("p t (m s) -> p m t s", s=PACK)
             pattern = "p (s m) t -> p m t s" if kind == "b" else "p (m s) t -> p m t s"
             dst = inter[kind, g, h][:].rearrange(pattern, s=PACK)
-            ms = slice(64 * part, 64 * (part + 1))
+            ms = slice(0, cut) if part == 0 else slice(cut, PART)
             copy(out=dst[:, ms], in_=src[:, ms])
 
         def quantize_inter(kind, g, h):
             src = inter[kind, g, h][:].rearrange("p n t -> p (n t)")
             (aq if kind == "a" else bq)[g, h] = quantize("%sq%d%d" % (kind, g, h), src)
 
+        d_all = kept("d_all", [PART, N], BF16)
+
+        def spread_d():
+            d_bank = bank(7)
+            d_words = d_rows[:].bitcast(F32)
+            for c in range(4):
+                nc.tensor.transpose(
+                    d_bank[:, PART * c : PART * (c + 1)], d_words[:, c : c + 1].to_broadcast([PART, PART]), ident[:]
+                )
+            nc.vector.tensor_copy(
+                out=d_all[:].bitcast(F32).rearrange("p (n c) -> p n c", c=4),
+                in_=d_bank[:].rearrange("p (c n) -> p n c", c=4),
+            )
         y_scales = kept("y_scales", [PART, N], U8)
         y_codes = {}
 
@@ -258,11 +270,7 @@ def tile_weighted_diis_error_k1_kernel(
             store_y(g, h, t)
 
         def store_y(g, h, t):
-            if t % 2 == 1:
-                pair = slice(t - 1, t + 1)
-                nc.sync.dma_start(
-                    out=by_slot(out_0, g)[:, pair, HALF * h : HALF * (h + 1)], in_=y_full[g, h][:, pair, :]
-                )
+            nc.sync.dma_start(out=by_slot(out_0, g)[:, t, HALF * h : HALF * (h + 1)], in_=y_full[g, h][:, t, :])
 
         def quantize_y(g, h):
             codes = kept("y_codes%d%d" % (g, h), [PART, HALF], U32)
@@ -310,24 +318,31 @@ def tile_weighted_diis_error_k1_kernel(
         for s in range(10):
             name, r0 = runs[s]
             turn_pair(name, r0, 2 * (s % 2))
-            if s == 2:
+            if s == 0:
+                spread_d()
                 nc.scalar.activation(out=omega_cols[:], in_=omega_bf[:], func=ACT.Copy)
                 nc.scalar.activation(out=omega_neg[:], in_=omega_bf[:], func=ACT.Copy, scale=-1.0)
+                for k in range(2):
+                    quantize_turned(name, k, 1)
             if s in act_extra:
                 interleave(*act_extra[s], nc.scalar.copy)
             if s < 8:
-                for k in range(2):
-                    scale_p(jobs[s][1] + k, jobs[s][2])
-                for k in range(2):
-                    quantize_turned(name, r0 + k)
+                j0, h = jobs[s][1:]
+                scale_p(j0, h, nc.vector, "pd", 4)
+                if s == 0:
+                    scale_p(j0 + 1, h, nc.vector, "pd", 4)
+            if s - 1 in act_extra and act_extra[s - 1][3] == 1:
+                quantize_inter(*act_extra[s - 1][:3])
+            if 0 < s < 8:
+                quantize_turned(name, r0, 2)
+                if True:
+                    scale_p(j0 + 1, h, nc.gpsimd, "turned%d" % (s % 3), 1)
             if s >= 1:
                 kind, j0, h = jobs[s - 1]
                 for k in range(2):
                     (product_a if kind == "a" else product_b)(j0 + k, h, 4 + 2 * (s % 2) + k)
                 for k in range(2):
                     (finish_a if kind == "a" else finish_b)(j0 + k, h)
-            if s in act_extra and act_extra[s][3] == 1:
-                quantize_inter(*act_extra[s][:3])
 
         act, vec = nc.scalar.copy, nc.vector.tensor_copy
         interleave("a", 1, 1, 1, act)
@@ -369,8 +384,8 @@ def tile_weighted_diis_error_k1_kernel(
         for t in range(2):
             weight_y(0, 0, t, omega_cols)
         quantize_inter("b", 0, 1)
-        interleave("b", 1, 1, 0, act)
-        interleave("b", 1, 1, 1, vec)
+        interleave("b", 1, 1, 0, act, 64)
+        interleave("b", 1, 1, 1, vec, 64)
         negate_l(1)
         quantize_inter("b", 1, 1)
         quantize_negated(1)
@@ -384,24 +399,24 @@ def tile_weighted_diis_error_k1_kernel(
             pass_bl(1, 0, t, 0)
         for t in range(PACK):
             pass_bl(1, 0, t, 1, stop=True)
-        interleave("y", 0, 0, 0, act)
         plain = staged("l_turned", [PART, PACK, HALF], F32, 2)
         for t in range(PACK):
             nc.scalar.copy(out=plain[:, t, :], in_=acc["y", 1, 0, t][:])
-        interleave("y", 0, 0, 1, vec)
+        interleave("y", 0, 0, 0, vec)
         for t in range(PACK):
             weight_plain(plain, 1, 0, t)
-        quantize_y(0, 0)
+        interleave("y", 0, 0, 1, vec)
         open_y(1, 1, 4)
-        for t in range(PACK):
+
+        def close_11(t):
             pass_lb(1, 1, t, 0, start=True)
             pass_lb(1, 1, t, 1)
-        for t in range(PACK):
             pass_bl(1, 1, t, 0)
             pass_bl(1, 1, t, 1, stop=True)
-        for part in range(2):
-            interleave("y", 1, 0, part, vec)
-        store_words(0, 0)
+
+        for t in range(2):
+            close_11(t)
+            weight_y(1, 1, t, omega_cols)
         open_y(0, 1, 0)
         for s in range(PACK):
             for t in range(PACK):
@@ -409,17 +424,22 @@ def tile_weighted_diis_error_k1_kernel(
                     acc["y", 0, 1, s][:, PART * t : PART * (t + 1)], plain[:, t, PART * s : PART * (s + 1)], ident[:]
                 )
         for t in range(PACK):
-            weight_y(1, 1, t, omega_cols)
-        for t in range(PACK):
             weight_y(0, 1, t, omega_neg)
-        interleave("y", 1, 1, 0, vec)
+        interleave("y", 1, 0, 0, vec)
+        quantize_y(0, 0)
+        interleave("y", 1, 0, 1, vec)
+        store_words(0, 0)
+        for t in range(2, PACK):
+            close_11(t)
+            weight_y(1, 1, t, omega_cols)
         quantize_y(1, 0)
-        interleave("y", 1, 1, 1, vec)
         store_words(1, 0)
-        quantize_y(1, 1)
-        store_words(1, 1)
         interleave("y", 0, 1, 0, vec)
         interleave("y", 0, 1, 1, vec)
+        interleave("y", 1, 1, 0, vec, 64)
+        interleave("y", 1, 1, 1, act, 64)
         quantize_y(0, 1)
         store_words(0, 1)
+        quantize_y(1, 1)
+        store_words(1, 1)
         store_scales()

@@ -73,8 +73,9 @@ def tile_weighted_diis_error_k1_kernel(
 
         load_p(0, 1)
         load_p(1, 1)
-        load_p(2, 2)
         load_w(0)
+        load_w(1)
+        load_p(2, 2)
         for q in range(4):
             nc.scalar.dma_start(
                 out=w_plane[32 * q : 32 * q + 4, :, :].bitcast(I32),
@@ -88,7 +89,6 @@ def tile_weighted_diis_error_k1_kernel(
         nc.gpsimd.dma_start(out=e_cols[:], in_=e.rearrange("(g p t) -> p g t", g=2, t=PACK))
         load_p(4, 2)
         load_p(6, 2)
-        load_w(1)
         raw = {}
         for name, mat in (("f", f_mat), ("l", l_mat)):
             for g in range(2):
@@ -142,17 +142,34 @@ def tile_weighted_diis_error_k1_kernel(
 
         def negate_l(h):
             neg = staged("l_neg", [PART, 2 * HALF * PACK], BF16, 1)
-            nc.vector.tensor_scalar(out=neg[:], in0=l_turned[h][:], scalar1=-1.0, scalar2=None, op0=ALU.mult)
             turned["n", h] = neg
+
+        def negate_cols(h, cols, on_scalar):
+            if on_scalar == "g":
+                nc.gpsimd.tensor_scalar(
+                    out=turned["n", h][:, cols], in0=l_turned[h][:, cols], scalar1=-1.0, scalar2=0.0, op0=ALU.mult, op1=ALU.add
+                )
+            elif on_scalar:
+                nc.scalar.activation(out=turned["n", h][:, cols], in_=l_turned[h][:, cols], func=ACT.Copy, scale=-1.0)
+            else:
+                nc.vector.tensor_scalar(
+                    out=turned["n", h][:, cols], in0=l_turned[h][:, cols], scalar1=-1.0, scalar2=None, op0=ALU.mult
+                )
 
         def quantize_negated(h):
             nlq[h] = quantize("nlq%d" % h, turned["n", h][:])
 
-        def scale_p(r, h, engine, tag, bufs):
+        for g in range(2):
+            for h in range(2):
+                a_full[g, h] = kept("a_full%d%d" % (g, h), [PART, PACK, HALF], F32)
+
+        def scale_p(r, h, slot=None):
             cols = slice(HALF * h, HALF * (h + 1))
-            prod = staged(tag, [PART, HALF], F32, bufs)
-            engine.tensor_tensor(out=prod[:], in0=p_raw[r][:, cols], in1=d_all[:, cols], op=ALU.mult)
-            pd[r, h] = prod
+            if slot is None:
+                engine, pd[r, h] = nc.vector, a_full[r // PACK, h][:, r % PACK, :]
+            else:
+                engine, pd[r, h] = nc.gpsimd, staged(slot, [PART, HALF], F32, 1)[:]
+            engine.tensor_tensor(out=pd[r, h], in0=p_raw[r][:, cols], in1=d_all[:, cols], op=ALU.mult)
 
         def mx(dst, lhs, lhs_col, rhs, rhs_col, start, stop):
             lcols = slice(lhs_col, lhs_col + PART)
@@ -184,9 +201,7 @@ def tile_weighted_diis_error_k1_kernel(
 
         def finish_a(r, h):
             g, t = divmod(r, PACK)
-            if t == 0:
-                a_full[g, h] = kept("a_full%d%d" % (g, h), [PART, PACK, HALF], F32)
-            nc.vector.tensor_tensor(out=a_full[g, h][:, t, :], in0=acc["a", r, h][:], in1=pd[r, h][:], op=ALU.add)
+            nc.vector.tensor_tensor(out=a_full[g, h][:, t, :], in0=acc["a", r, h][:], in1=pd[r, h], op=ALU.add)
 
         def product_b(r, h, index):
             dst = bank(index)
@@ -210,11 +225,26 @@ def tile_weighted_diis_error_k1_kernel(
         def interleave(kind, g, h, part, copy, cut=64):
             if part == 0:
                 inter[kind, g, h] = staged("inter", [PART, HALF, PACK], BF16, 4)
-            src = {"a": a_full, "b": b_rows, "y": y_full}[kind][g, h][:].rearrange("p t (m s) -> p m t s", s=PACK)
-            pattern = "p (s m) t -> p m t s" if kind == "b" else "p (m s) t -> p m t s"
-            dst = inter[kind, g, h][:].rearrange(pattern, s=PACK)
-            ms = slice(0, cut) if part == 0 else slice(cut, PART)
+            if kind == "b":
+                src = b_rows[g, h][:].rearrange("p t (n i s) -> p n s i t", i=2, s=PACK)
+                dst = inter[kind, g, h][:].rearrange("p (s n i) t -> p n s i t", i=2, s=PACK)
+                ms = slice(0, cut // 2) if part == 0 else slice(cut // 2, PART // 2)
+            else:
+                src = (a_full if kind == "a" else y_full)[g, h][:].rearrange("p t (m s) -> p m t s", s=PACK)
+                dst = inter[kind, g, h][:].rearrange("p (m s) t -> p m t s", s=PACK)
+                ms = slice(0, cut) if part == 0 else slice(cut, PART)
             copy(out=dst[:, ms], in_=src[:, ms])
+
+        def interleave_on_gpsimd(g, h):
+            inter["a", g, h] = staged("inter", [PART, HALF, PACK], BF16, 4)
+            nc.gpsimd.tensor_scalar(
+                out=inter["a", g, h][:],
+                in0=a_full[g, h][:].rearrange("p t n -> p n t"),
+                scalar1=1.0,
+                scalar2=0.0,
+                op0=ALU.mult,
+                op1=ALU.add,
+            )
 
         def quantize_inter(kind, g, h):
             src = inter[kind, g, h][:].rearrange("p n t -> p (n t)")
@@ -295,11 +325,9 @@ def tile_weighted_diis_error_k1_kernel(
                 )
 
         runs = [(name, 2 * j) for name in "pfl" for j in range(4)]
-        jobs = [("a", 2 * j, 0) for j in range(4)] + [("a", 2 * j, 1) for j in range(4)] + [("b", 0, 0)]
-        act_extra = {
-            3: ("a", 0, 0, 0), 4: ("a", 0, 0, 1), 5: ("a", 1, 0, 0), 6: ("a", 1, 0, 1),
-            7: ("a", 0, 1, 0), 8: ("a", 0, 1, 1), 9: ("a", 1, 1, 0),
-        }
+        jobs = [((0, 0), (0, 1)), ((1, 0), (1, 1))]
+        jobs += [((r, h), (r + 1, h)) for r, h in ((2, 0), (4, 0), (6, 0), (2, 1), (4, 1), (6, 1))]
+        act_extra = {3: ("a", 0, 0, 0), 4: ("a", 0, 0, 1), 5: ("a", 1, 0, 0), 6: ("a", 1, 0, 1), 7: ("a", 0, 1, 0), 8: ("a", 0, 1, 1)}
 
         def turn_pair(name, r0, first):
             for k in range(2):
@@ -315,61 +343,69 @@ def tile_weighted_diis_error_k1_kernel(
             for k in range(2):
                 finish_b(r0 + k, h)
 
+        spread_d()
         for s in range(10):
             name, r0 = runs[s]
             turn_pair(name, r0, 2 * (s % 2))
             if s == 0:
-                spread_d()
                 nc.scalar.activation(out=omega_cols[:], in_=omega_bf[:], func=ACT.Copy)
                 nc.scalar.activation(out=omega_neg[:], in_=omega_bf[:], func=ACT.Copy, scale=-1.0)
-                for k in range(2):
-                    quantize_turned(name, k, 1)
+                for r, h in jobs[0]:
+                    scale_p(r, h)
+                quantize_turned(name, 0, 1)
+                scale_p(1, 0)
+                quantize_turned(name, 1, 1)
+                scale_p(1, 1)
             if s in act_extra:
-                interleave(*act_extra[s], nc.scalar.copy)
-            if s < 8:
-                j0, h = jobs[s][1:]
-                scale_p(j0, h, nc.vector, "pd", 4)
-                if s == 0:
-                    scale_p(j0 + 1, h, nc.vector, "pd", 4)
-            if s - 1 in act_extra and act_extra[s - 1][3] == 1:
-                quantize_inter(*act_extra[s - 1][:3])
+                interleave(*act_extra[s], nc.vector.tensor_copy if s in (4,) else nc.scalar.copy)
+            if 0 < s < 7 and jobs[s + 1][0] not in pd:
+                scale_p(*jobs[s + 1][0])
+            if s == 1:
+                scale_p(2, 1)
+            if s in (5, 7):
+                quantize_inter("a", (s - 5) // 2, 0)
+            if s == 8:
+                interleave_on_gpsimd(1, 1)
             if 0 < s < 8:
                 quantize_turned(name, r0, 2)
-                if True:
-                    scale_p(j0 + 1, h, nc.gpsimd, "turned%d" % (s % 3), 1)
-            if s >= 1:
-                kind, j0, h = jobs[s - 1]
-                for k in range(2):
-                    (product_a if kind == "a" else product_b)(j0 + k, h, 4 + 2 * (s % 2) + k)
-                for k in range(2):
-                    (finish_a if kind == "a" else finish_b)(j0 + k, h)
+            if 0 < s < 7:
+                scale_p(*jobs[s + 1][1], "turned%d" % (s % 3))
+            if s < 8:
+                for k, (r, h) in enumerate(jobs[s]):
+                    product_a(r, h, 4 + 2 * (s % 2) + k)
+                for r, h in jobs[s]:
+                    finish_a(r, h)
+            else:
+                b_pair(2 * (s - 8), 0, 4 + 2 * (s % 2))
+                finish_b_pair(2 * (s - 8), 0)
 
         act, vec = nc.scalar.copy, nc.vector.tensor_copy
-        interleave("a", 1, 1, 1, act)
-        b_pair(2, 0, 4)
-        finish_b_pair(2, 0)
-        b_pair(4, 0, 6)
+        b_pair(4, 0, 4)
         interleave("b", 0, 0, 0, act)
         interleave("b", 0, 0, 1, act)
         finish_b_pair(4, 0)
+        quantize_inter("a", 0, 1)
         quantize_inter("a", 1, 1)
-        b_pair(6, 0, 0)
+        b_pair(6, 0, 6)
         finish_b_pair(6, 0)
+        turn_pair("l", 4, 0)
         interleave("b", 1, 0, 0, act)
         interleave("b", 1, 0, 1, act)
-        turn_pair("l", 4, 2)
         b_pair(0, 1, 4)
+        turn_pair("l", 6, 2)
         b_pair(2, 1, 6)
-        turn_pair("l", 6, 0)
         negate_l(0)
+        negate_cols(0, slice(0, 4096), False)
         quantize_l(0)
         quantize_inter("b", 0, 0)
         quantize_negated(0)
         quantize_inter("b", 1, 0)
+        negate_l(1)
+        negate_cols(1, slice(0, 2048), True)
         finish_b_pair(0, 1)
         finish_b_pair(2, 1)
-        b_pair(4, 1, 2)
-        b_pair(6, 1, 0)
+        b_pair(4, 1, 0)
+        b_pair(6, 1, 2)
         interleave("b", 0, 1, 0, act)
         interleave("b", 0, 1, 1, act)
         open_y(0, 0, 4)
@@ -386,7 +422,7 @@ def tile_weighted_diis_error_k1_kernel(
         quantize_inter("b", 0, 1)
         interleave("b", 1, 1, 0, act, 64)
         interleave("b", 1, 1, 1, vec, 64)
-        negate_l(1)
+        negate_cols(1, slice(2048, 4096), False)
         quantize_inter("b", 1, 1)
         quantize_negated(1)
         for t in range(2, PACK):

@@ -19,13 +19,16 @@ ACT = mybir.ActivationFunctionType
 PART = 128
 PACK = 4
 HALF = 512
-TILES = 8
+QUADS = PART
+TURN_RING = 4
+LAST_B_CUT = 48
 
 
 def tile_weighted_diis_error_k1_kernel(
     tc, p_mat, w_words, w_scales, d, f_mat, e, l_mat, omega, out_0, out_1, out_2
 ):
     nc = tc.nc
+    on_scalar, on_vector = nc.scalar.copy, nc.vector.tensor_copy
     with ExitStack() as ctx:
         keep = ctx.enter_context(tc.tile_pool(name="keep", bufs=1))
         work = ctx.enter_context(tc.tile_pool(name="work", bufs=2))
@@ -41,8 +44,11 @@ def tile_weighted_diis_error_k1_kernel(
         def bank(index):
             return psum.tile([PART, HALF], F32, name="bank%d" % index, tag="bank%d" % index)
 
-        def by_slot(mat, g):
+        def row_tiles(mat, g):
             return mat[HALF * g : HALF * (g + 1), :].rearrange("(p t) k -> p t k", t=PACK)
+
+        def half(h):
+            return slice(HALF * h, HALF * (h + 1))
 
         def quantize(name, src):
             width = src.shape[1] // PACK
@@ -54,32 +60,24 @@ def tile_weighted_diis_error_k1_kernel(
         d_rows = kept("d_rows", [PART, 8], BF16)
         nc.scalar.dma_start(out=d_rows[:], in_=d.rearrange("(p c) -> p c", c=8))
         w_plane = kept("w_plane", [PART, 2, N], U8)
-        nc.vector.memset(w_plane[:].rearrange("p g n -> p (g n)").bitcast(I32), 0)
-        w_codes = [kept("w_codes%d" % h, [PART, 2, N], U8) for h in range(2)]
+        nc.vector.memset(w_plane[:].rearrange("p c n -> p (c n)").bitcast(I32), 0)
         p_raw = {}
 
         def load_p(r0, count):
             rows = kept("p_raw%d" % r0, [PART, count, N], BF16)
             g, t = divmod(r0, PACK)
-            nc.sync.dma_start(out=rows[:], in_=by_slot(p_mat, g)[:, t : t + count, :])
+            nc.sync.dma_start(out=rows[:], in_=row_tiles(p_mat, g)[:, t : t + count, :])
             for k in range(count):
                 p_raw[r0 + k] = rows[:, k, :]
 
-        def load_w(h):
-            nc.sync.dma_start(
-                out=w_codes[h][:].bitcast(I32),
-                in_=w_words.rearrange("g p n -> p g n")[:, :, N * h : N * (h + 1)].bitcast(I32),
-            )
-
         load_p(0, 1)
         load_p(1, 1)
-        load_w(0)
-        load_w(1)
-        load_p(2, 2)
+        w_codes = kept("w_codes", [PART, 2, 2 * N], U8)
+        nc.sync.dma_start(out=w_codes[:].bitcast(I32), in_=w_words.rearrange("c p n -> p c n").bitcast(I32))
         for q in range(4):
             nc.scalar.dma_start(
                 out=w_plane[32 * q : 32 * q + 4, :, :].bitcast(I32),
-                in_=w_scales.rearrange("g r n -> r g n")[4 * q : 4 * q + 4, :, :].bitcast(I32),
+                in_=w_scales.rearrange("c r n -> r c n")[4 * q : 4 * q + 4, :, :].bitcast(I32),
             )
         ident = kept("ident", [PART, PART], F32)
         make_identity(nc, ident[:])
@@ -87,327 +85,268 @@ def tile_weighted_diis_error_k1_kernel(
         nc.gpsimd.dma_start(out=omega_bf[:], in_=omega.rearrange("(g p t) -> p g t", g=2, t=PACK))
         e_cols = kept("e_cols", [PART, 2, PACK], BF16)
         nc.gpsimd.dma_start(out=e_cols[:], in_=e.rearrange("(g p t) -> p g t", g=2, t=PACK))
-        load_p(4, 2)
-        load_p(6, 2)
+        for r0 in (2, 4, 6):
+            load_p(r0, 2)
         raw = {}
         for name, mat in (("f", f_mat), ("l", l_mat)):
             for g in range(2):
-                slab = staged("slab", [PART, PACK, N], BF16, 4)
-                nc.sync.dma_start(out=slab[:], in_=by_slot(mat, g))
-                raw[name, g] = slab
+                raw[name, g] = staged("slab", [PART, PACK, N], BF16, 4)
+                nc.sync.dma_start(out=raw[name, g][:], in_=row_tiles(mat, g))
 
-        omega_cols = kept("omega_cols", [PART, 2, PACK], F32)
+        omega_pos = kept("omega_pos", [PART, 2, PACK], F32)
         omega_neg = kept("omega_neg", [PART, 2, PACK], F32)
+        d_all = kept("d_all", [PART, N], BF16)
+        a_full = {
+            (g, h): kept("a_full%d%d" % (g, h), [PART, PACK, HALF], F32) for g in range(2) for h in range(2)
+        }
+        y_scales = kept("y_scales", [PART, N], U8)
 
-        turned, pq, fq, lq, nlq, aq, bq = {}, {}, {}, {}, {}, {}, {}
-        pd, acc, a_full, b_rows, inter, l_turned, y_full = {}, {}, {}, {}, {}, {}, {}
+        sums = {}
+        turned, l_turned, l_negated = {}, {}, {}
+        left, lq, nlq, aq, bq, y_codes = {}, {}, {}, {}, {}, {}
+        pd, b_rows, y_full, inter = {}, {}, {}, {}
 
-        def raw_rows(name, r):
-            return p_raw[r] if name == "p" else raw[name, r // PACK][:, r % PACK, :]
-
-        def turn(name, r, index):
-            words = raw_rows(name, r).bitcast(F32)
-            dst = bank(index)
-            for c in range(2):
-                for u in range(2):
-                    j = 2 * c + u
-                    nc.tensor.transpose(
-                        dst[:, PART * j : PART * (j + 1)], words[:, 256 * c + u : 256 * (c + 1) : 2], ident[:]
-                    )
-            acc["t", name, r] = dst
-
-        def empty_turned(name, r):
-            src = acc["t", name, r][:].rearrange("p (c u m) -> p c m u", c=2, u=2)
-            if name == "l":
-                h, t = divmod(r, PACK)
-                if t == 0:
-                    l_turned[h] = staged("l_turned", [PART, 2 * HALF * PACK], BF16, 2)
-                dst = l_turned[h][:].bitcast(F32).rearrange("p (c t m u) -> p t c m u", c=2, t=PACK, u=2)[:, t]
-            else:
-                if r % 2 == 0:
-                    turned[name, r // 2] = staged("turned%d" % ((r // 2 + (4 if name == "f" else 0)) % 3), [PART, 4 * PART * PACK], BF16, 1)
-                dst = turned[name, r // 2][:].bitcast(F32).rearrange("p (k c m u) -> p k c m u", k=2, c=2, u=2)[:, r % 2]
-            nc.scalar.copy(out=dst, in_=src)
-
-        def quantize_turned(name, r0, count):
-            k0 = r0 % 2
-            src = turned[name, r0 // 2][:, 2 * PART * PACK * k0 : 2 * PART * PACK * (k0 + count)]
-            codes, scales = quantize("%sq%d" % (name, r0), src)
-            for k in range(count):
-                cols = slice(2 * PART * k, 2 * PART * (k + 1))
-                (pq if name == "p" else fq)[r0 + k] = (codes[:, cols], scales[:, cols])
-
-        def quantize_l(h):
-            lq[h] = quantize("lq%d" % h, l_turned[h][:])
-
-        def negate_l(h):
-            neg = staged("l_neg", [PART, 2 * HALF * PACK], BF16, 1)
-            turned["n", h] = neg
-
-        def negate_cols(h, cols, on_scalar):
-            if on_scalar == "g":
-                nc.gpsimd.tensor_scalar(
-                    out=turned["n", h][:, cols], in0=l_turned[h][:, cols], scalar1=-1.0, scalar2=0.0, op0=ALU.mult, op1=ALU.add
+        def spread_d():
+            dst = bank(7)
+            words = d_rows[:].bitcast(F32)
+            for c in range(4):
+                nc.tensor.transpose(
+                    dst[:, PART * c : PART * (c + 1)], words[:, c : c + 1].to_broadcast([PART, PART]), ident[:]
                 )
-            elif on_scalar:
-                nc.scalar.activation(out=turned["n", h][:, cols], in_=l_turned[h][:, cols], func=ACT.Copy, scale=-1.0)
+            on_vector(
+                out=d_all[:].bitcast(F32).rearrange("p (n c) -> p n c", c=4),
+                in_=dst[:].rearrange("p (c n) -> p n c", c=4),
+            )
+
+        def turn_tag(step, k):
+            return "turned%d_%d" % (step % TURN_RING, k)
+
+        def turn_pair(name, r0, first_bank, step=None):
+            banks = []
+            for r in (r0, r0 + 1):
+                rows = p_raw[r] if name == "p" else raw[name, r // PACK][:, r % PACK, :]
+                words = rows.bitcast(F32)
+                dst = bank(first_bank + r - r0)
+                for c in range(2):
+                    for u in range(2):
+                        cols = slice(PART * (2 * c + u), PART * (2 * c + u + 1))
+                        nc.tensor.transpose(dst[:, cols], words[:, 256 * c + u : 256 * (c + 1) : 2], ident[:])
+                banks.append(dst)
+            for r, src in zip((r0, r0 + 1), banks):
+                if name == "l":
+                    g, t = divmod(r, PACK)
+                    if t == 0:
+                        l_turned[g] = staged("l_turned", [PART, 2 * HALF * PACK], BF16, 2)
+                    dst = l_turned[g][:].bitcast(F32).rearrange("p (c t m u) -> p t c m u", c=2, t=PACK, u=2)[:, t]
+                else:
+                    turned[name, r] = staged(turn_tag(step, r - r0), [PART, 2 * PART * PACK], BF16, 1)
+                    dst = turned[name, r][:].bitcast(F32).rearrange("p (c m u) -> p c m u", c=2, u=2)
+                on_scalar(out=dst, in_=src[:].rearrange("p (c u m) -> p c m u", c=2, u=2))
+
+        def quantize_turned(name, r):
+            left[name, r] = quantize("%sq%d" % (name, r), turned[name, r][:])
+
+        def quantize_l(g):
+            lq[g] = quantize("lq%d" % g, l_turned[g][:])
+
+        def negate_l(g, c0, c1, scalar_engine=False):
+            if c0 == 0:
+                l_negated[g] = staged("l_negated", [PART, 2 * HALF * PACK], BF16, 1)
+            cols = slice(HALF * PACK * c0, HALF * PACK * c1)
+            src, dst = l_turned[g][:, cols], l_negated[g][:, cols]
+            if scalar_engine:
+                nc.scalar.activation(out=dst, in_=src, func=ACT.Copy, scale=-1.0)
             else:
-                nc.vector.tensor_scalar(
-                    out=turned["n", h][:, cols], in0=l_turned[h][:, cols], scalar1=-1.0, scalar2=None, op0=ALU.mult
-                )
+                nc.vector.tensor_scalar(out=dst, in0=src, scalar1=-1.0, scalar2=None, op0=ALU.mult)
 
-        def quantize_negated(h):
-            nlq[h] = quantize("nlq%d" % h, turned["n", h][:])
+        def quantize_negated(g):
+            nlq[g] = quantize("nlq%d" % g, l_negated[g][:])
 
-        for g in range(2):
-            for h in range(2):
-                a_full[g, h] = kept("a_full%d%d" % (g, h), [PART, PACK, HALF], F32)
-
-        def scale_p(r, h, slot=None):
-            cols = slice(HALF * h, HALF * (h + 1))
-            if slot is None:
+        def scale_p(r, h, gpsimd_tag=None):
+            if gpsimd_tag is None:
                 engine, pd[r, h] = nc.vector, a_full[r // PACK, h][:, r % PACK, :]
             else:
-                engine, pd[r, h] = nc.gpsimd, staged(slot, [PART, HALF], F32, 1)[:]
-            engine.tensor_tensor(out=pd[r, h], in0=p_raw[r][:, cols], in1=d_all[:, cols], op=ALU.mult)
+                engine, pd[r, h] = nc.gpsimd, staged(gpsimd_tag, [PART, HALF], F32, 1)[:]
+            engine.tensor_tensor(out=pd[r, h], in0=p_raw[r][:, half(h)], in1=d_all[:, half(h)], op=ALU.mult)
 
-        def mx(dst, lhs, lhs_col, rhs, rhs_col, start, stop):
-            lcols = slice(lhs_col, lhs_col + PART)
-            rcols = slice(rhs_col, rhs_col + HALF)
+        def mx(dst, lhs, lhs_col, rhs_codes, rhs_scales, start, stop):
+            cols = slice(lhs_col, lhs_col + PART)
             nc.tensor.matmul_mx(
                 out=dst[:],
-                lhsT=lhs[0][:, lcols].bitcast(FP8X4),
-                lhsT_scale=lhs[1][:, lcols],
-                rhs=rhs[0][:, rcols].bitcast(FP8X4),
-                rhs_scale=rhs[1][:, rcols],
+                lhsT=lhs[0][:, cols].bitcast(FP8X4),
+                lhsT_scale=lhs[1][:, cols],
+                rhs=rhs_codes,
+                rhs_scale=rhs_scales,
                 start=start,
                 stop=stop,
             )
 
-        def product_a(r, h, index):
-            dst = bank(index)
-            for c in range(2):
-                lcols = slice(PART * c, PART * (c + 1))
-                nc.tensor.matmul_mx(
-                    out=dst[:],
-                    lhsT=pq[r][0][:, lcols].bitcast(FP8X4),
-                    lhsT_scale=pq[r][1][:, lcols],
-                    rhs=w_codes[h][:, c, :].bitcast(FP4X4),
-                    rhs_scale=w_plane[:, c, HALF * h : HALF * (h + 1)],
-                    start=(c == 0),
-                    stop=(c == 1),
+        def moving(operand, part):
+            return operand[0][:, half(part)].bitcast(FP8X4), operand[1][:, half(part)]
+
+        def a_pair(jobs, first_bank):
+            for k, (r, h) in enumerate(jobs):
+                sums["a", r, h] = bank(first_bank + k)
+                for c in range(2):
+                    codes = w_codes[:, c, N * h : N * (h + 1)].bitcast(FP4X4)
+                    mx(sums["a", r, h], left["p", r], PART * c, codes, w_plane[:, c, half(h)], c == 0, c == 1)
+            for r, h in jobs:
+                nc.vector.tensor_tensor(
+                    out=a_full[r // PACK, h][:, r % PACK, :], in0=sums["a", r, h][:], in1=pd[r, h], op=ALU.add
                 )
-            acc["a", r, h] = dst
 
-        def finish_a(r, h):
-            g, t = divmod(r, PACK)
-            nc.vector.tensor_tensor(out=a_full[g, h][:, t, :], in0=acc["a", r, h][:], in1=pd[r, h], op=ALU.add)
+        def b_products(r0, h, first_bank):
+            for r in (r0, r0 + 1):
+                sums["b", r, h] = bank(first_bank + r - r0)
+                for c in range(2):
+                    mx(sums["b", r, h], left["f", r], PART * c, *moving(aq[c, h], 0), c == 0, c == 1)
 
-        def product_b(r, h, index):
-            dst = bank(index)
-            for c in range(2):
-                mx(dst, fq[r], PART * c, aq[c, h], 0, c == 0, c == 1)
-            acc["b", r, h] = dst
+        def b_finish(r0, h):
+            for r in (r0, r0 + 1):
+                g, t = divmod(r, PACK)
+                if t == 0:
+                    b_rows[g, h] = staged("b_rows", [PART, PACK, HALF], BF16, 2)
+                nc.vector.scalar_tensor_tensor(
+                    out=b_rows[g, h][:, t, :],
+                    in0=a_full[g, h][:, t, :],
+                    scalar=e_cols[:, g, t : t + 1],
+                    in1=sums["b", r, h][:],
+                    op0=ALU.mult,
+                    op1=ALU.add,
+                )
 
-        def finish_b(r, h):
-            g, t = divmod(r, PACK)
-            if t == 0:
-                b_rows[g, h] = staged("b_rows", [PART, PACK, HALF], BF16, 2)
-            nc.vector.scalar_tensor_tensor(
-                out=b_rows[g, h][:, t, :],
-                in0=a_full[g, h][:, t, :],
-                scalar=e_cols[:, g, t : t + 1],
-                in1=acc["b", r, h][:],
-                op0=ALU.mult,
-                op1=ALU.add,
-            )
-
-        def interleave(kind, g, h, part, copy, cut=64):
-            if part == 0:
+        def interleave(kind, g, h, copy, lo=0, hi=QUADS):
+            if lo == 0:
                 inter[kind, g, h] = staged("inter", [PART, HALF, PACK], BF16, 4)
             if kind == "b":
                 src = b_rows[g, h][:].rearrange("p t (n i s) -> p n s i t", i=2, s=PACK)
                 dst = inter[kind, g, h][:].rearrange("p (s n i) t -> p n s i t", i=2, s=PACK)
-                ms = slice(0, cut // 2) if part == 0 else slice(cut // 2, PART // 2)
+                part = slice(lo // 2, hi // 2)
             else:
                 src = (a_full if kind == "a" else y_full)[g, h][:].rearrange("p t (m s) -> p m t s", s=PACK)
                 dst = inter[kind, g, h][:].rearrange("p (m s) t -> p m t s", s=PACK)
-                ms = slice(0, cut) if part == 0 else slice(cut, PART)
-            copy(out=dst[:, ms], in_=src[:, ms])
-
-        def interleave_on_gpsimd(g, h):
-            inter["a", g, h] = staged("inter", [PART, HALF, PACK], BF16, 4)
-            nc.gpsimd.tensor_scalar(
-                out=inter["a", g, h][:],
-                in0=a_full[g, h][:].rearrange("p t n -> p n t"),
-                scalar1=1.0,
-                scalar2=0.0,
-                op0=ALU.mult,
-                op1=ALU.add,
-            )
+                part = slice(lo, hi)
+            copy(out=dst[:, part], in_=src[:, part])
 
         def quantize_inter(kind, g, h):
             src = inter[kind, g, h][:].rearrange("p n t -> p (n t)")
             (aq if kind == "a" else bq)[g, h] = quantize("%sq%d%d" % (kind, g, h), src)
 
-        d_all = kept("d_all", [PART, N], BF16)
-
-        def spread_d():
-            d_bank = bank(7)
-            d_words = d_rows[:].bitcast(F32)
-            for c in range(4):
-                nc.tensor.transpose(
-                    d_bank[:, PART * c : PART * (c + 1)], d_words[:, c : c + 1].to_broadcast([PART, PART]), ident[:]
-                )
-            nc.vector.tensor_copy(
-                out=d_all[:].bitcast(F32).rearrange("p (n c) -> p n c", c=4),
-                in_=d_bank[:].rearrange("p (c n) -> p n c", c=4),
-            )
-        y_scales = kept("y_scales", [PART, N], U8)
-        y_codes = {}
-
-        def open_y(g, h, first):
+        def open_y(g, h, first_bank):
             for t in range(PACK):
-                acc["y", g, h, t] = bank(first + t)
+                sums["y", g, h, t] = bank(first_bank + t)
 
         def pass_lb(g, h, t, c, start=False, stop=False):
-            mx(acc["y", g, h, t], lq[g], HALF * c + PART * t, bq[c, h], 0, start, stop)
+            mx(sums["y", g, h, t], lq[g], HALF * c + PART * t, *moving(bq[c, h], 0), start, stop)
 
         def pass_bl(g, h, t, c, start=False, stop=False):
-            mx(acc["y", g, h, t], bq[c, g], PART * t, nlq[h], HALF * c, start, stop)
+            mx(sums["y", g, h, t], bq[c, g], PART * t, *moving(nlq[h], c), start, stop)
 
-        def weight_y(g, h, t, weights):
+        def y_rows(g, h, t):
             if t == 0:
                 y_full[g, h] = staged("slab", [PART, PACK, HALF], F32, 4)
+            return y_full[g, h][:, t, :]
+
+        def store_y(g, h, t):
+            nc.sync.dma_start(out=row_tiles(out_0, g)[:, t, half(h)], in_=y_full[g, h][:, t, :])
+
+        def weight_y(g, h, t, weights):
             nc.scalar.activation(
-                out=y_full[g, h][:, t, :].rearrange("p (m s) -> p m s", s=PACK),
-                in_=acc["y", g, h, t][:].rearrange("p (s m) -> p m s", s=PACK),
+                out=y_rows(g, h, t).rearrange("p (m s) -> p m s", s=PACK),
+                in_=sums["y", g, h, t][:].rearrange("p (s m) -> p m s", s=PACK),
                 func=ACT.Copy,
                 scale=weights[:, g, t : t + 1],
             )
             store_y(g, h, t)
 
-        def weight_plain(plain, g, h, t):
-            if t == 0:
-                y_full[g, h] = staged("slab", [PART, PACK, HALF], F32, 4)
+        def weight_unweighted(src, g, h, t):
             nc.vector.tensor_scalar(
-                out=y_full[g, h][:, t, :].rearrange("p (n i s) -> p n s i", i=2, s=PACK),
-                in0=plain[:, t, :].rearrange("p (s n i) -> p n s i", i=2, s=PACK),
-                scalar1=omega_cols[:, g, t : t + 1],
+                out=y_rows(g, h, t).rearrange("p (n i s) -> p n s i", i=2, s=PACK),
+                in0=src[:, t, :].rearrange("p (s n i) -> p n s i", i=2, s=PACK),
+                scalar1=omega_pos[:, g, t : t + 1],
                 scalar2=None,
                 op0=ALU.mult,
             )
             store_y(g, h, t)
 
-        def store_y(g, h, t):
-            nc.sync.dma_start(out=by_slot(out_0, g)[:, t, HALF * h : HALF * (h + 1)], in_=y_full[g, h][:, t, :])
-
         def quantize_y(g, h):
-            codes = kept("y_codes%d%d" % (g, h), [PART, HALF], U32)
+            y_codes[g, h] = kept("y_codes%d%d" % (g, h), [PART, HALF], U32)
             nc.vector.quantize_mx(
-                out=codes[:].bitcast(FP8X4),
-                scales=y_scales[4 * g :, HALF * h : HALF * (h + 1)],
+                out=y_codes[g, h][:].bitcast(FP8X4),
+                scales=y_scales[4 * g :, half(h)],
                 in_=inter["y", g, h][:].rearrange("p n t -> p (n t)"),
             )
-            y_codes[g, h] = codes
 
         def store_words(g, h):
-            words = out_1[g].rearrange("p m t -> p (m t)")
-            nc.sync.dma_start(
-                out=words[:, PACK * HALF * h : PACK * HALF * (h + 1)].bitcast(I32), in_=y_codes[g, h][:].bitcast(I32)
-            )
+            words = out_1[g].rearrange("p m t -> p (m t)")[:, PACK * HALF * h : PACK * HALF * (h + 1)]
+            nc.sync.dma_start(out=words.bitcast(I32), in_=y_codes[g, h][:].bitcast(I32))
 
-        def store_scales():
-            for q in range(4):
-                (nc.sync if q % 2 == 0 else nc.scalar).dma_start(
-                    out=out_2[:, 4 * q : 4 * q + 4, :].bitcast(I32),
-                    in_=y_scales[32 * q : 32 * q + 8, :].bitcast(I32),
-                )
-
-        runs = [(name, 2 * j) for name in "pfl" for j in range(4)]
+        pairs = [(name, r0) for name in "pf" for r0 in (0, 2, 4, 6)] + [("l", 0), ("l", 2)]
         jobs = [((0, 0), (0, 1)), ((1, 0), (1, 1))]
-        jobs += [((r, h), (r + 1, h)) for r, h in ((2, 0), (4, 0), (6, 0), (2, 1), (4, 1), (6, 1))]
-        act_extra = {3: ("a", 0, 0, 0), 4: ("a", 0, 0, 1), 5: ("a", 1, 0, 0), 6: ("a", 1, 0, 1), 7: ("a", 0, 1, 0), 8: ("a", 0, 1, 1)}
+        jobs = jobs + [((r, h), (r + 1, h)) for h in range(2) for r in (2, 4, 6)]
+        a_quadrants = ((0, 0), (1, 0), (0, 1), (1, 1))
+        first_a_step = 3
 
-        def turn_pair(name, r0, first):
-            for k in range(2):
-                turn(name, r0 + k, first + k)
-            for k in range(2):
-                empty_turned(name, r0 + k)
-
-        def b_pair(r0, h, first):
-            for k in range(2):
-                product_b(r0 + k, h, first + k)
-
-        def finish_b_pair(r0, h):
-            for k in range(2):
-                finish_b(r0 + k, h)
+        vector_scales = {1: ((2, 1), (3, 1)), 3: ((6, 0),), 6: ((6, 1),)}
+        gpsimd_scales = dict(enumerate([(r, h) for h in range(2) for r in (4, 5, 7)], 1))
 
         spread_d()
-        for s in range(10):
-            name, r0 = runs[s]
-            turn_pair(name, r0, 2 * (s % 2))
-            if s == 0:
-                nc.scalar.activation(out=omega_cols[:], in_=omega_bf[:], func=ACT.Copy)
+        for step, (name, r0) in enumerate(pairs):
+            turn_pair(name, r0, 2 * (step % 2), step)
+            if step == 0:
+                nc.scalar.activation(out=omega_pos[:], in_=omega_bf[:], func=ACT.Copy)
                 nc.scalar.activation(out=omega_neg[:], in_=omega_bf[:], func=ACT.Copy, scale=-1.0)
-                for r, h in jobs[0]:
-                    scale_p(r, h)
-                quantize_turned(name, 0, 1)
+                scale_p(0, 0)
+                scale_p(0, 1)
+                quantize_turned(name, 0)
                 scale_p(1, 0)
-                quantize_turned(name, 1, 1)
+                quantize_turned(name, 1)
                 scale_p(1, 1)
-            if s in act_extra:
-                interleave(*act_extra[s], nc.vector.tensor_copy if s in (4,) else nc.scalar.copy)
-            if 0 < s < 7 and jobs[s + 1][0] not in pd:
-                scale_p(*jobs[s + 1][0])
-            if s == 1:
-                scale_p(2, 1)
-            if s in (5, 7):
-                quantize_inter("a", (s - 5) // 2, 0)
-            if s == 8:
-                interleave_on_gpsimd(1, 1)
-            if 0 < s < 8:
-                quantize_turned(name, r0, 2)
-            if 0 < s < 7:
-                scale_p(*jobs[s + 1][1], "turned%d" % (s % 3))
-            if s < 8:
-                for k, (r, h) in enumerate(jobs[s]):
-                    product_a(r, h, 4 + 2 * (s % 2) + k)
-                for r, h in jobs[s]:
-                    finish_a(r, h)
+                scale_p(2, 0)
+                scale_p(3, 0)
+            quadrant, part = divmod(step - first_a_step, 2)
+            if step >= first_a_step:
+                interleave("a", *a_quadrants[quadrant], on_scalar, QUADS // 2 * part, QUADS // 2 * (part + 1))
+            for r, h in vector_scales.get(step, ()):
+                scale_p(r, h)
+            if quadrant >= 1 and part == 0:
+                quantize_inter("a", *a_quadrants[quadrant - 1])
+            if step == len(pairs) - 1:
+                interleave("a", 1, 1, on_vector, QUADS // 2, QUADS)
+            if step > 0 and name != "l":
+                quantize_turned(name, r0 + 1)
+                quantize_turned(name, r0)
+            if step in gpsimd_scales:
+                scale_p(*gpsimd_scales[step], turn_tag(step, 1))
+            if step < len(jobs):
+                a_pair(jobs[step], 4 + 2 * (step % 2))
             else:
-                b_pair(2 * (s - 8), 0, 4 + 2 * (s % 2))
-                finish_b_pair(2 * (s - 8), 0)
+                b_products(r0, 0, 4 + 2 * (step % 2))
+                b_finish(r0, 0)
 
-        act, vec = nc.scalar.copy, nc.vector.tensor_copy
-        b_pair(4, 0, 4)
-        interleave("b", 0, 0, 0, act)
-        interleave("b", 0, 0, 1, act)
-        finish_b_pair(4, 0)
-        quantize_inter("a", 0, 1)
+        b_products(4, 0, 4)
+        interleave("b", 0, 0, on_scalar)
+        b_finish(4, 0)
         quantize_inter("a", 1, 1)
-        b_pair(6, 0, 6)
-        finish_b_pair(6, 0)
+        b_products(6, 0, 6)
+        b_finish(6, 0)
         turn_pair("l", 4, 0)
-        interleave("b", 1, 0, 0, act)
-        interleave("b", 1, 0, 1, act)
-        b_pair(0, 1, 4)
+        interleave("b", 1, 0, on_scalar)
+        b_products(0, 1, 4)
         turn_pair("l", 6, 2)
-        b_pair(2, 1, 6)
-        negate_l(0)
-        negate_cols(0, slice(0, 4096), False)
+        b_products(2, 1, 6)
+        negate_l(0, 0, 2)
         quantize_l(0)
         quantize_inter("b", 0, 0)
         quantize_negated(0)
         quantize_inter("b", 1, 0)
-        negate_l(1)
-        negate_cols(1, slice(0, 2048), True)
-        finish_b_pair(0, 1)
-        finish_b_pair(2, 1)
-        b_pair(4, 1, 0)
-        b_pair(6, 1, 2)
-        interleave("b", 0, 1, 0, act)
-        interleave("b", 0, 1, 1, act)
+        negate_l(1, 0, 1, scalar_engine=True)
+        b_finish(0, 1)
+        b_finish(2, 1)
+        b_products(4, 1, 0)
+        b_products(6, 1, 2)
+        interleave("b", 0, 1, on_scalar)
+
         open_y(0, 0, 4)
         for t in range(PACK):
             pass_lb(0, 0, t, 0, start=True)
@@ -415,18 +354,18 @@ def tile_weighted_diis_error_k1_kernel(
             pass_lb(0, 0, t, 1)
             pass_bl(0, 0, t, 1, stop=True)
         quantize_l(1)
-        finish_b_pair(4, 1)
-        finish_b_pair(6, 1)
-        for t in range(2):
-            weight_y(0, 0, t, omega_cols)
+        b_finish(4, 1)
+        b_finish(6, 1)
+        weight_y(0, 0, 0, omega_pos)
         quantize_inter("b", 0, 1)
-        interleave("b", 1, 1, 0, act, 64)
-        interleave("b", 1, 1, 1, vec, 64)
-        negate_cols(1, slice(2048, 4096), False)
+        interleave("b", 1, 1, on_scalar, 0, LAST_B_CUT)
+        interleave("b", 1, 1, on_vector, LAST_B_CUT, QUADS)
+        negate_l(1, 1, 2)
         quantize_inter("b", 1, 1)
         quantize_negated(1)
-        for t in range(2, PACK):
-            weight_y(0, 0, t, omega_cols)
+        for t in range(1, PACK):
+            weight_y(0, 0, t, omega_pos)
+
         open_y(1, 0, 0)
         for t in range(PACK):
             pass_lb(1, 0, t, 0, start=True)
@@ -435,47 +374,51 @@ def tile_weighted_diis_error_k1_kernel(
             pass_bl(1, 0, t, 0)
         for t in range(PACK):
             pass_bl(1, 0, t, 1, stop=True)
-        plain = staged("l_turned", [PART, PACK, HALF], F32, 2)
+        unweighted = staged("l_turned", [PART, PACK, HALF], F32, 2)
         for t in range(PACK):
-            nc.scalar.copy(out=plain[:, t, :], in_=acc["y", 1, 0, t][:])
-        interleave("y", 0, 0, 0, vec)
+            on_scalar(out=unweighted[:, t, :], in_=sums["y", 1, 0, t][:])
+        interleave("y", 0, 0, on_vector, 0, QUADS // 2)
         for t in range(PACK):
-            weight_plain(plain, 1, 0, t)
-        interleave("y", 0, 0, 1, vec)
+            weight_unweighted(unweighted, 1, 0, t)
+        interleave("y", 0, 0, on_vector, QUADS // 2, QUADS)
+
         open_y(1, 1, 4)
 
-        def close_11(t):
+        def finish_last(t):
             pass_lb(1, 1, t, 0, start=True)
             pass_lb(1, 1, t, 1)
             pass_bl(1, 1, t, 0)
             pass_bl(1, 1, t, 1, stop=True)
+            weight_y(1, 1, t, omega_pos)
 
         for t in range(2):
-            close_11(t)
-            weight_y(1, 1, t, omega_cols)
+            finish_last(t)
         open_y(0, 1, 0)
         for s in range(PACK):
             for t in range(PACK):
                 nc.tensor.transpose(
-                    acc["y", 0, 1, s][:, PART * t : PART * (t + 1)], plain[:, t, PART * s : PART * (s + 1)], ident[:]
+                    sums["y", 0, 1, s][:, PART * t : PART * (t + 1)],
+                    unweighted[:, t, PART * s : PART * (s + 1)],
+                    ident[:],
                 )
         for t in range(PACK):
             weight_y(0, 1, t, omega_neg)
-        interleave("y", 1, 0, 0, vec)
+        interleave("y", 1, 0, on_vector, 0, QUADS // 2)
         quantize_y(0, 0)
-        interleave("y", 1, 0, 1, vec)
+        interleave("y", 1, 0, on_vector, QUADS // 2, QUADS)
         store_words(0, 0)
         for t in range(2, PACK):
-            close_11(t)
-            weight_y(1, 1, t, omega_cols)
+            finish_last(t)
         quantize_y(1, 0)
         store_words(1, 0)
-        interleave("y", 0, 1, 0, vec)
-        interleave("y", 0, 1, 1, vec)
-        interleave("y", 1, 1, 0, vec, 64)
-        interleave("y", 1, 1, 1, act, 64)
-        quantize_y(0, 1)
-        store_words(0, 1)
-        quantize_y(1, 1)
-        store_words(1, 1)
-        store_scales()
+        interleave("y", 0, 1, on_vector)
+        interleave("y", 1, 1, on_vector, 0, QUADS // 2)
+        interleave("y", 1, 1, on_scalar, QUADS // 2, QUADS)
+        for g in range(2):
+            quantize_y(g, 1)
+            store_words(g, 1)
+        for q in range(4):
+            (nc.sync if q % 2 == 0 else nc.scalar).dma_start(
+                out=out_2[:, 4 * q : 4 * q + 4, :].bitcast(I32),
+                in_=y_scales[32 * q : 32 * q + 8, :].bitcast(I32),
+            )

from contextlib import ExitStack

import concourse.mybir as mybir
from concourse.masks import make_identity

N = 1024
FLOPS = 3 * 2 * N * N * N

F32 = mybir.dt.float32
BF16 = mybir.dt.bfloat16
I32 = mybir.dt.int32
U32 = mybir.dt.uint32
U8 = mybir.dt.uint8
FP8X4 = mybir.dt.float8_e4m3fn_x4
FP4X4 = mybir.dt.float4_e2m1fn_x4
ALU = mybir.AluOpType
ACT = mybir.ActivationFunctionType

PART = 128
PACK = 4
HALF = 512
QUADS = PART
TURN_RING = 4
LAST_B_CUT = 48


def tile_weighted_diis_error_k1_kernel(
    tc, p_mat, w_words, w_scales, d, f_mat, e, l_mat, omega, out_0, out_1, out_2
):
    nc = tc.nc
    on_scalar, on_vector = nc.scalar.copy, nc.vector.tensor_copy
    with ExitStack() as ctx:
        keep = ctx.enter_context(tc.tile_pool(name="keep", bufs=1))
        work = ctx.enter_context(tc.tile_pool(name="work", bufs=2))
        psum = ctx.enter_context(tc.psum_pool(name="psum", bufs=1))
        ctx.enter_context(tc.manual_schedule())

        def kept(name, shape, dtype):
            return keep.tile(shape, dtype, name=name, align_bytes=64)

        def staged(tag, shape, dtype, bufs):
            return work.tile(shape, dtype, name=tag, tag=tag, bufs=bufs, align_bytes=64)

        def bank(index):
            return psum.tile([PART, HALF], F32, name="bank%d" % index, tag="bank%d" % index)

        def row_tiles(mat, g):
            return mat[HALF * g : HALF * (g + 1), :].rearrange("(p t) k -> p t k", t=PACK)

        def half(h):
            return slice(HALF * h, HALF * (h + 1))

        def quantize(name, src):
            width = src.shape[1] // PACK
            codes = kept(name + "_codes", [PART, width], U32)
            scales = kept(name + "_scales", [PART, width], U8)
            nc.vector.quantize_mx(out=codes[:].bitcast(FP8X4), scales=scales[:], in_=src)
            return codes, scales

        d_rows = kept("d_rows", [PART, 8], BF16)
        nc.scalar.dma_start(out=d_rows[:], in_=d.rearrange("(p c) -> p c", c=8))
        w_plane = kept("w_plane", [PART, 2, N], U8)
        nc.vector.memset(w_plane[:].rearrange("p c n -> p (c n)").bitcast(I32), 0)
        p_raw = {}

        def load_p(r0, count):
            rows = kept("p_raw%d" % r0, [PART, count, N], BF16)
            g, t = divmod(r0, PACK)
            nc.sync.dma_start(out=rows[:], in_=row_tiles(p_mat, g)[:, t : t + count, :])
            for k in range(count):
                p_raw[r0 + k] = rows[:, k, :]

        load_p(0, 1)
        load_p(1, 1)
        w_codes = kept("w_codes", [PART, 2, 2 * N], U8)
        nc.sync.dma_start(out=w_codes[:].bitcast(I32), in_=w_words.rearrange("c p n -> p c n").bitcast(I32))
        for q in range(4):
            nc.scalar.dma_start(
                out=w_plane[32 * q : 32 * q + 4, :, :].bitcast(I32),
                in_=w_scales.rearrange("c r n -> r c n")[4 * q : 4 * q + 4, :, :].bitcast(I32),
            )
        ident = kept("ident", [PART, PART], F32)
        make_identity(nc, ident[:])
        omega_bf = kept("omega_bf", [PART, 2, PACK], BF16)
        nc.gpsimd.dma_start(out=omega_bf[:], in_=omega.rearrange("(g p t) -> p g t", g=2, t=PACK))
        e_cols = kept("e_cols", [PART, 2, PACK], BF16)
        nc.gpsimd.dma_start(out=e_cols[:], in_=e.rearrange("(g p t) -> p g t", g=2, t=PACK))
        for r0 in (2, 4, 6):
            load_p(r0, 2)
        raw = {}
        for name, mat in (("f", f_mat), ("l", l_mat)):
            for g in range(2):
                raw[name, g] = staged("slab", [PART, PACK, N], BF16, 4)
                nc.sync.dma_start(out=raw[name, g][:], in_=row_tiles(mat, g))

        omega_pos = kept("omega_pos", [PART, 2, PACK], F32)
        omega_neg = kept("omega_neg", [PART, 2, PACK], F32)
        d_all = kept("d_all", [PART, N], BF16)
        a_full = {
            (g, h): kept("a_full%d%d" % (g, h), [PART, PACK, HALF], F32) for g in range(2) for h in range(2)
        }
        y_scales = kept("y_scales", [PART, N], U8)

        sums = {}
        turned, l_turned, l_negated = {}, {}, {}
        left, lq, nlq, aq, bq, y_codes = {}, {}, {}, {}, {}, {}
        pd, b_rows, y_full, inter = {}, {}, {}, {}

        def spread_d():
            dst = bank(7)
            words = d_rows[:].bitcast(F32)
            for c in range(4):
                nc.tensor.transpose(
                    dst[:, PART * c : PART * (c + 1)], words[:, c : c + 1].to_broadcast([PART, PART]), ident[:]
                )
            on_vector(
                out=d_all[:].bitcast(F32).rearrange("p (n c) -> p n c", c=4),
                in_=dst[:].rearrange("p (c n) -> p n c", c=4),
            )

        def turn_tag(step, k):
            return "turned%d_%d" % (step % TURN_RING, k)

        def turn_pair(name, r0, first_bank, step=None):
            banks = []
            for r in (r0, r0 + 1):
                rows = p_raw[r] if name == "p" else raw[name, r // PACK][:, r % PACK, :]
                words = rows.bitcast(F32)
                dst = bank(first_bank + r - r0)
                for c in range(2):
                    for u in range(2):
                        cols = slice(PART * (2 * c + u), PART * (2 * c + u + 1))
                        nc.tensor.transpose(dst[:, cols], words[:, 256 * c + u : 256 * (c + 1) : 2], ident[:])
                banks.append(dst)
            for r, src in zip((r0, r0 + 1), banks):
                if name == "l":
                    g, t = divmod(r, PACK)
                    if t == 0:
                        l_turned[g] = staged("l_turned", [PART, 2 * HALF * PACK], BF16, 2)
                    dst = l_turned[g][:].bitcast(F32).rearrange("p (c t m u) -> p t c m u", c=2, t=PACK, u=2)[:, t]
                else:
                    turned[name, r] = staged(turn_tag(step, r - r0), [PART, 2 * PART * PACK], BF16, 1)
                    dst = turned[name, r][:].bitcast(F32).rearrange("p (c m u) -> p c m u", c=2, u=2)
                on_scalar(out=dst, in_=src[:].rearrange("p (c u m) -> p c m u", c=2, u=2))

        def quantize_turned(name, r):
            left[name, r] = quantize("%sq%d" % (name, r), turned[name, r][:])

        def quantize_l(g):
            lq[g] = quantize("lq%d" % g, l_turned[g][:])

        def negate_l(g, c0, c1, scalar_engine=False):
            if c0 == 0:
                l_negated[g] = staged("l_negated", [PART, 2 * HALF * PACK], BF16, 1)
            cols = slice(HALF * PACK * c0, HALF * PACK * c1)
            src, dst = l_turned[g][:, cols], l_negated[g][:, cols]
            if scalar_engine:
                nc.scalar.activation(out=dst, in_=src, func=ACT.Copy, scale=-1.0)
            else:
                nc.vector.tensor_scalar(out=dst, in0=src, scalar1=-1.0, scalar2=None, op0=ALU.mult)

        def quantize_negated(g):
            nlq[g] = quantize("nlq%d" % g, l_negated[g][:])

        def scale_p(r, h, gpsimd_tag=None):
            if gpsimd_tag is None:
                engine, pd[r, h] = nc.vector, a_full[r // PACK, h][:, r % PACK, :]
            else:
                engine, pd[r, h] = nc.gpsimd, staged(gpsimd_tag, [PART, HALF], F32, 1)[:]
            engine.tensor_tensor(out=pd[r, h], in0=p_raw[r][:, half(h)], in1=d_all[:, half(h)], op=ALU.mult)

        def mx(dst, lhs, lhs_col, rhs_codes, rhs_scales, start, stop):
            cols = slice(lhs_col, lhs_col + PART)
            nc.tensor.matmul_mx(
                out=dst[:],
                lhsT=lhs[0][:, cols].bitcast(FP8X4),
                lhsT_scale=lhs[1][:, cols],
                rhs=rhs_codes,
                rhs_scale=rhs_scales,
                start=start,
                stop=stop,
            )

        def moving(operand, part):
            return operand[0][:, half(part)].bitcast(FP8X4), operand[1][:, half(part)]

        def a_pair(jobs, first_bank):
            for k, (r, h) in enumerate(jobs):
                sums["a", r, h] = bank(first_bank + k)
                for c in range(2):
                    codes = w_codes[:, c, N * h : N * (h + 1)].bitcast(FP4X4)
                    mx(sums["a", r, h], left["p", r], PART * c, codes, w_plane[:, c, half(h)], c == 0, c == 1)
            for r, h in jobs:
                nc.vector.tensor_tensor(
                    out=a_full[r // PACK, h][:, r % PACK, :], in0=sums["a", r, h][:], in1=pd[r, h], op=ALU.add
                )

        def b_products(r0, h, first_bank):
            for r in (r0, r0 + 1):
                sums["b", r, h] = bank(first_bank + r - r0)
                for c in range(2):
                    mx(sums["b", r, h], left["f", r], PART * c, *moving(aq[c, h], 0), c == 0, c == 1)

        def b_finish(r0, h):
            for r in (r0, r0 + 1):
                g, t = divmod(r, PACK)
                if t == 0:
                    b_rows[g, h] = staged("b_rows", [PART, PACK, HALF], BF16, 2)
                nc.vector.scalar_tensor_tensor(
                    out=b_rows[g, h][:, t, :],
                    in0=a_full[g, h][:, t, :],
                    scalar=e_cols[:, g, t : t + 1],
                    in1=sums["b", r, h][:],
                    op0=ALU.mult,
                    op1=ALU.add,
                )

        def interleave(kind, g, h, copy, lo=0, hi=QUADS):
            if lo == 0:
                inter[kind, g, h] = staged("inter", [PART, HALF, PACK], BF16, 4)
            if kind == "b":
                src = b_rows[g, h][:].rearrange("p t (n i s) -> p n s i t", i=2, s=PACK)
                dst = inter[kind, g, h][:].rearrange("p (s n i) t -> p n s i t", i=2, s=PACK)
                part = slice(lo // 2, hi // 2)
            else:
                src = (a_full if kind == "a" else y_full)[g, h][:].rearrange("p t (m s) -> p m t s", s=PACK)
                dst = inter[kind, g, h][:].rearrange("p (m s) t -> p m t s", s=PACK)
                part = slice(lo, hi)
            copy(out=dst[:, part], in_=src[:, part])

        def quantize_inter(kind, g, h):
            src = inter[kind, g, h][:].rearrange("p n t -> p (n t)")
            (aq if kind == "a" else bq)[g, h] = quantize("%sq%d%d" % (kind, g, h), src)

        def open_y(g, h, first_bank):
            for t in range(PACK):
                sums["y", g, h, t] = bank(first_bank + t)

        def pass_lb(g, h, t, c, start=False, stop=False):
            mx(sums["y", g, h, t], lq[g], HALF * c + PART * t, *moving(bq[c, h], 0), start, stop)

        def pass_bl(g, h, t, c, start=False, stop=False):
            mx(sums["y", g, h, t], bq[c, g], PART * t, *moving(nlq[h], c), start, stop)

        def y_rows(g, h, t):
            if t == 0:
                y_full[g, h] = staged("slab", [PART, PACK, HALF], F32, 4)
            return y_full[g, h][:, t, :]

        def store_y(g, h, t):
            nc.sync.dma_start(out=row_tiles(out_0, g)[:, t, half(h)], in_=y_full[g, h][:, t, :])

        def weight_y(g, h, t, weights):
            nc.scalar.activation(
                out=y_rows(g, h, t).rearrange("p (m s) -> p m s", s=PACK),
                in_=sums["y", g, h, t][:].rearrange("p (s m) -> p m s", s=PACK),
                func=ACT.Copy,
                scale=weights[:, g, t : t + 1],
            )
            store_y(g, h, t)

        def weight_unweighted(src, g, h, t):
            nc.vector.tensor_scalar(
                out=y_rows(g, h, t).rearrange("p (n i s) -> p n s i", i=2, s=PACK),
                in0=src[:, t, :].rearrange("p (s n i) -> p n s i", i=2, s=PACK),
                scalar1=omega_pos[:, g, t : t + 1],
                scalar2=None,
                op0=ALU.mult,
            )
            store_y(g, h, t)

        def quantize_y(g, h):
            y_codes[g, h] = kept("y_codes%d%d" % (g, h), [PART, HALF], U32)
            nc.vector.quantize_mx(
                out=y_codes[g, h][:].bitcast(FP8X4),
                scales=y_scales[4 * g :, half(h)],
                in_=inter["y", g, h][:].rearrange("p n t -> p (n t)"),
            )

        def store_words(g, h):
            words = out_1[g].rearrange("p m t -> p (m t)")[:, PACK * HALF * h : PACK * HALF * (h + 1)]
            nc.sync.dma_start(out=words.bitcast(I32), in_=y_codes[g, h][:].bitcast(I32))

        pairs = [(name, r0) for name in "pf" for r0 in (0, 2, 4, 6)] + [("l", 0), ("l", 2)]
        jobs = [((0, 0), (0, 1)), ((1, 0), (1, 1))]
        jobs = jobs + [((r, h), (r + 1, h)) for h in range(2) for r in (2, 4, 6)]
        a_quadrants = ((0, 0), (1, 0), (0, 1), (1, 1))
        first_a_step = 3

        vector_scales = {1: ((2, 1), (3, 1)), 3: ((6, 0),), 6: ((6, 1),)}
        gpsimd_scales = dict(enumerate([(r, h) for h in range(2) for r in (4, 5, 7)], 1))

        spread_d()
        for step, (name, r0) in enumerate(pairs):
            turn_pair(name, r0, 2 * (step % 2), step)
            if step == 0:
                nc.scalar.activation(out=omega_pos[:], in_=omega_bf[:], func=ACT.Copy)
                nc.scalar.activation(out=omega_neg[:], in_=omega_bf[:], func=ACT.Copy, scale=-1.0)
                scale_p(0, 0)
                scale_p(0, 1)
                quantize_turned(name, 0)
                scale_p(1, 0)
                quantize_turned(name, 1)
                scale_p(1, 1)
                scale_p(2, 0)
                scale_p(3, 0)
            quadrant, part = divmod(step - first_a_step, 2)
            if step >= first_a_step:
                interleave("a", *a_quadrants[quadrant], on_scalar, QUADS // 2 * part, QUADS // 2 * (part + 1))
            for r, h in vector_scales.get(step, ()):
                scale_p(r, h)
            if quadrant >= 1 and part == 0:
                quantize_inter("a", *a_quadrants[quadrant - 1])
            if step == len(pairs) - 1:
                interleave("a", 1, 1, on_vector, QUADS // 2, QUADS)
            if step > 0 and name != "l":
                quantize_turned(name, r0 + 1)
                quantize_turned(name, r0)
            if step in gpsimd_scales:
                scale_p(*gpsimd_scales[step], turn_tag(step, 1))
            if step < len(jobs):
                a_pair(jobs[step], 4 + 2 * (step % 2))
            else:
                b_products(r0, 0, 4 + 2 * (step % 2))
                b_finish(r0, 0)

        b_products(4, 0, 4)
        interleave("b", 0, 0, on_scalar)
        b_finish(4, 0)
        quantize_inter("a", 1, 1)
        b_products(6, 0, 6)
        b_finish(6, 0)
        turn_pair("l", 4, 0)
        interleave("b", 1, 0, on_scalar)
        b_products(0, 1, 4)
        turn_pair("l", 6, 2)
        b_products(2, 1, 6)
        negate_l(0, 0, 2)
        quantize_l(0)
        quantize_inter("b", 0, 0)
        quantize_negated(0)
        quantize_inter("b", 1, 0)
        negate_l(1, 0, 1, scalar_engine=True)
        b_finish(0, 1)
        b_finish(2, 1)
        b_products(4, 1, 0)
        b_products(6, 1, 2)
        interleave("b", 0, 1, on_scalar)

        open_y(0, 0, 4)
        for t in range(PACK):
            pass_lb(0, 0, t, 0, start=True)
            pass_bl(0, 0, t, 0)
            pass_lb(0, 0, t, 1)
            pass_bl(0, 0, t, 1, stop=True)
        quantize_l(1)
        b_finish(4, 1)
        b_finish(6, 1)
        weight_y(0, 0, 0, omega_pos)
        quantize_inter("b", 0, 1)
        interleave("b", 1, 1, on_scalar, 0, LAST_B_CUT)
        interleave("b", 1, 1, on_vector, LAST_B_CUT, QUADS)
        negate_l(1, 1, 2)
        quantize_inter("b", 1, 1)
        quantize_negated(1)
        for t in range(1, PACK):
            weight_y(0, 0, t, omega_pos)

        open_y(1, 0, 0)
        for t in range(PACK):
            pass_lb(1, 0, t, 0, start=True)
            pass_lb(1, 0, t, 1)
        for t in range(PACK):
            pass_bl(1, 0, t, 0)
        for t in range(PACK):
            pass_bl(1, 0, t, 1, stop=True)
        unweighted = staged("l_turned", [PART, PACK, HALF], F32, 2)
        for t in range(PACK):
            on_scalar(out=unweighted[:, t, :], in_=sums["y", 1, 0, t][:])
        interleave("y", 0, 0, on_vector, 0, QUADS // 2)
        for t in range(PACK):
            weight_unweighted(unweighted, 1, 0, t)
        interleave("y", 0, 0, on_vector, QUADS // 2, QUADS)

        open_y(1, 1, 4)

        def finish_last(t):
            pass_lb(1, 1, t, 0, start=True)
            pass_lb(1, 1, t, 1)
            pass_bl(1, 1, t, 0)
            pass_bl(1, 1, t, 1, stop=True)
            weight_y(1, 1, t, omega_pos)

        for t in range(2):
            finish_last(t)
        open_y(0, 1, 0)
        for s in range(PACK):
            for t in range(PACK):
                nc.tensor.transpose(
                    sums["y", 0, 1, s][:, PART * t : PART * (t + 1)],
                    unweighted[:, t, PART * s : PART * (s + 1)],
                    ident[:],
                )
        for t in range(PACK):
            weight_y(0, 1, t, omega_neg)
        interleave("y", 1, 0, on_vector, 0, QUADS // 2)
        quantize_y(0, 0)
        interleave("y", 1, 0, on_vector, QUADS // 2, QUADS)
        store_words(0, 0)
        for t in range(2, PACK):
            finish_last(t)
        quantize_y(1, 0)
        store_words(1, 0)
        interleave("y", 0, 1, on_vector)
        interleave("y", 1, 1, on_vector, 0, QUADS // 2)
        interleave("y", 1, 1, on_scalar, QUADS // 2, QUADS)
        for g in range(2):
            quantize_y(g, 1)
            store_words(g, 1)
        for q in range(4):
            (nc.sync if q % 2 == 0 else nc.scalar).dma_start(
                out=out_2[:, 4 * q : 4 * q + 4, :].bitcast(I32),
                in_=y_scales[32 * q : 32 * q + 8, :].bitcast(I32),
            )
